import numpy as np, ml_dtypes
CORES = [2,3,42,43,82,83,122,123]
N = 8
BF = ml_dtypes.bfloat16
T, R, S, H, CAP = 256, 64, 9, 4096, 1280
U, A, M, B0 = T // R, CAP // 16, max(T, CAP // 4), ((H + 1) << S) // 8191 + 1
def keys(x, hc):
    X = np.ascontiguousarray(x.transpose(1, 0, 2)).reshape(128, N * T).astype(np.int64); h = hc[0].astype(np.int64)
    before = np.concatenate([np.zeros((128, 1), np.int64), X[:, :-1]], axis=1)
    return X, ((h[:, :1] * before + h[:, 1:] * X) >> S) & (H - 1)
def stretches(v):
    return np.ascontiguousarray(v.reshape(128, N, T).transpose(1, 0, 2)).astype(np.float32)
def multipliers(rng):
    return np.stack([rng.integers(1, 1024, 128), rng.integers(B0, (1 << S) + 1, 128)], axis=1)
def keyset(rng, n):
    return np.argsort(rng.random((128, n)), axis=-1)[:, :M]
def pools(rng, K):
    return np.take_along_axis(np.broadcast_to(K, (N,) + K.shape), np.argsort(rng.random((N,) + K.shape), axis=-1), axis=-1)
def counts(rng):
    d = rng.integers(0, A - R + 1, (N, 64)); return np.stack([A + d, A - d], axis=2).reshape(N, 128)
def uneven(rng, n):
    v = np.concatenate([[T], R + n // 15 + (np.arange(15) < n % 15)])
    return rng.permuted(np.broadcast_to(v, (N, 8, 16)).copy(), axis=-1).reshape(N, 128)
def order(rng, D, P, pin=False):
    i = np.arange(P.shape[-1]); e = rng.random((N, 128, U, P.shape[-1]), dtype=np.float32)
    b = rng.permuted(np.broadcast_to(np.arange(U), (N, 128, U)).copy(), axis=-1)[..., None]
    e = e - (i // R == b) + 4 * (i >= D[:, :, None, None])
    if pin: e[..., 0] = -9; e[..., 1] = -8
    o = np.argsort(e, axis=-1)[..., :R]
    if pin: o = np.concatenate([o[..., :1], rng.permuted(o[..., 2:], axis=-1), o[..., 1:2]], axis=-1)
    else: o = rng.permuted(o, axis=-1)
    return np.take_along_axis(np.broadcast_to(P[:, :, None], (N, 128, U, P.shape[-1])), o, axis=-1).reshape(N, 128, T)
def spell(rng, k, h):
    kk = k.transpose(1, 0, 2).reshape(128, N * T).astype(np.int64); X = np.zeros((128, N * T), np.int64); coin = rng.random((128, N * T)); up = rng.random((128, N * T)) < 0.5; last = np.zeros(128, np.int64); a, b = h[:, 0], h[:, 1]
    for t in range(N * T):
        w = ((kk[:, t] << S) - a * last) & ((H << S) - 1); w2 = w + (H << S)
        w = np.where(up[:, t] & ((w2 + (1 << S) - 1) // b <= 8191), w2, w); lo = (w + b - 1) // b; hi = (w + (1 << S) - 1) // b
        last = lo + np.floor(coin[:, t] * (hi - lo + 1)).astype(np.int64); X[:, t] = last
    return {"x": np.ascontiguousarray(X.reshape(128, N, T).transpose(1, 0, 2)).astype(np.int32), "hc": np.broadcast_to(h, (N, 128, 2)).astype(np.int32)}
def setup_inputs(rng):
    D = np.maximum(R, counts(rng) - rng.integers(0, 5, (N, 128)))
    return spell(rng, order(rng, D, pools(rng, keyset(rng, H))), multipliers(rng))
def setup_inputs_full(rng):
    D = np.where(np.arange(128) // 16 % 2 == 0, uneven(rng, CAP - T - 15 * R), counts(rng))
    P = pools(rng, keyset(rng, H)); P[:, ::3] = np.stack([keyset(rng, H)[::3] for r in range(N)])
    return spell(rng, order(rng, D, P), multipliers(rng))
def setup_inputs_ends(rng):
    P = pools(rng, keyset(rng, H - 2) + 1); P[..., 0] = 0; P[..., 1] = H - 1
    k = order(rng, counts(rng), P, True).reshape(N, 128, U, R); k[:, ::2, 1::2, 0] = H - 1; k[:, ::2, 1::2, R - 1] = 0
    k[0, 1::4, 0, R - 1] = k[0, 1::4, 0, 1]; k[0, 1::4, 0, 0] = H - 1; k[0, 1::4, 0, 1] = 0
    h = multipliers(rng); h[1::4, 0] = 0
    d = spell(rng, k.reshape(N, 128, T), h); d["x"][0, 1::4, 1] = 0; return d
def setup_inputs_far(rng):
    K = keyset(rng, H); P = pools(rng, K[:, M // 2:]); Q = pools(rng, K[:, :M // 2]); P[0] = Q[0]; P[N - 1] = Q[N - 1]; P[N - 1, ::2] = Q[0, ::2]
    D = counts(rng); D[N - 1] = D[0]
    return spell(rng, order(rng, D, P), multipliers(rng))
def setup_inputs_same(rng):
    K = keyset(rng, H); k = order(rng, np.full((N, 128), R), np.broadcast_to(K, (N,) + K.shape))
    k[:, 1::2] = np.tile(k[0, 1::2, :R], (1, U)); return spell(rng, k, multipliers(rng))
def setup_inputs_spread(rng):
    K = (rng.integers(0, H, (128, 1)) + np.arange(M)) % H
    h = np.stack([rng.choice(np.array([0, 1, 1023]), 128), rng.choice(np.array([B0, 1 << S]), 128)], axis=1)
    return spell(rng, order(rng, uneven(rng, 0), pools(rng, K)), h)
def check_inputs(d):
    bad = []; x, hc = d["x"], d["hc"]
    if not (x.min() >= 0 and x.max() <= 8191): bad.append("tokens")
    if not (hc[..., 0].min() >= 0 and hc[..., 0].max() <= 1023 and hc[..., 1].min() >= 1 and hc[..., 1].max() <= 1 << S): bad.append("multipliers")
    if (hc != hc[:1]).any(): bad.append("hc_alike")
    k = keys(x, hc)[1].reshape(128, N, T).transpose(1, 0, 2)
    s = np.sort(k.reshape(N, 128, U, R), axis=-1)
    if (s[..., 1:] == s[..., :-1]).any(): bad.append("runs")
    s = np.sort(k, axis=-1); n = 1 + np.sum(s[..., 1:] != s[..., :-1], axis=-1)
    if np.sum(n.reshape(N, 8, 16), axis=-1).max() > CAP: bad.append("new_keys")
    return bad
def reference(x, hc):
    X, k = keys(x, hc); L = N * T
    u = (np.arange(128)[:, None] * H + k).reshape(-1); o = np.argsort(u, kind="stable")
    same = u[o[1:]] == u[o[:-1]]
    prev = np.full(128 * L, -1, np.int64); prev[o[1:][same]] = o[:-1][same] % L
    prev = prev.reshape(128, L); after = np.where(prev >= 0, np.take_along_axis(X, prev + 1, axis=1), -1)
    return {"y": stretches(prev), "z": stretches(after)}

@@ -1,0 +1,474 @@
+from concourse.bass import DstId, RemoteDMATransfer
+from concourse.mybir import AluOpType, ActivationFunctionType
+
+N, T_, R, H = 8, 256, 64, 4096
+NU = N * T_ // R
+NK = NU // 2
+COPY = ActivationFunctionType.Copy
+BF = "bfloat16"
+REST = [(t, c) for t in range(2) for c in range(8)][1:]
+NV, NF, NS, NA, NG = 5, 3, 7, 2, 1
+VF, AF, GF, DF = REST[:NV], REST[NV:NV + NS], REST[NV + NS:NV + NS + NG], REST[NV + NS + NG:]
+
+SCRATCH = {
+    "xs": ("dram", [8, 128, 32], "int32"),
+    "d1": ("dram", [8, 128, 32], "int32"),
+    "xd": ("dram", [8, 128, 64], BF),
+    "d2": ("dram", [8, 128, 64], BF),
+    "dy": ("dram", [8, 128, 64], "float32"),
+    "dy1": ("dram", [8, 128, 32], "float32"),
+    "dy2": ("dram", [8, 128, 32], "float32"),
+    "xq": ("sbuf", [128, 256], "int32"),
+    "xh": ("sbuf", [128, 256], BF), "xl": ("sbuf", [128, 256], BF),
+    "lnd": ("sbuf", [128, 256], "int32"),
+    "tt": ("sbuf", [128, 8, 2, 16], "int32"),
+    "xf": ("sbuf", [128, 2, 144], "float32"),
+    "jj": ("sbuf", [128, 128], "float32"),
+    "j16": ("sbuf", [128, 128], "float32"),
+    "cl": ("sbuf", [128, 128], "float32"),
+    "sel": ("sbuf", [128, 128], "float32"),
+    "hs": ("sbuf", [128, 4], "int32"),
+    "hsf": ("sbuf", [128, 4], "float32"),
+    "abf": ("sbuf", [128, 4], "float32"),
+    "m0": ("sbuf", [128, 128], "float32"),
+    "m1": ("sbuf", [128, 128], "float32"),
+    "mw": ("sbuf", [128, 128], "float32"),
+    "ta": ("sbuf", [128, 2, 128], "float32"),
+    "tb": ("sbuf", [128, 2, 128], "float32"),
+    "mm": ("sbuf", [128, 2, 128], "float32"),
+    "ww": ("sbuf", [128, 2, 128], "float32"),
+    "dm": ("sbuf", [128, 128], "float32"),
+    "pi": ("sbuf", [128, 8], "int32"), "p7": ("sbuf", [128, 8], "int32"), "pr": ("sbuf", [128, 8], "float32"),
+    "li": ("sbuf", [128, 256], BF), "rb": ("sbuf", [128, 256], BF),
+    "on": ("sbuf", [128, 2, 8], BF), "w0": ("sbuf", [128, 2, 8], BF),
+    "w1": ("sbuf", [128, 2, 8], BF), "w2": ("sbuf", [128, 2, 8], BF),
+    "ee": ("sbuf", [128, 2, 144], BF),
+    "vv": ("sbuf", [128, 2048], BF),
+    "ki": ("sbuf", [128, 2, 16, 8], "int32"), "kj": ("sbuf", [128, 2, 16, 8], "int32"),
+    "ll": ("sbuf", [128, 2, 17, 16], "uint16"),
+    "win0": ("sbuf", [128, 2 * H], BF), "win1": ("sbuf", [128, 2 * H], BF),
+    "gg": ("sbuf", [128, 2, 4096], BF),
+    "c1": ("sbuf", [128, 2, 64], "float32"),
+    "cm": ("sbuf", [128, 2, 64], "float32"),
+    "cs": ("sbuf", [128, 8, 64], "float32"),
+    "cs1": ("sbuf", [128, 32], "float32"),
+    "cs2": ("sbuf", [128, 32], "float32"),
+    "ab": ("psum", [128, 512], "float32"), "pz": ("psum", [128, 512], "float32"),
+    "ps": ("psum", [128, 2, 256], "float32"),
+    "qa": ("psum", [128, 512], "float32"), "qb": ("psum", [128, 512], "float32"),
+    "u0": ("psum", [128, 512], "float32"), "u1": ("psum", [128, 512], "float32"), "u2": ("psum", [128, 512], "float32"),
+}
+SEMAPHORES = (["x1", "x2", "hcl", "lka", "lkb", "snt", "rin", "rin1", "rin2",
+               "ij", "ipi", "ij16", "ili", "gw", "gl", "ifl", "fdm", "vi", "seed", "rdy", "pab", "abd", "msk", "cst", "mats",
+               "edn", "ddn", "sfl", "gz", "dgh", "dgl", "xds", "vz", "rbd", "pl", "xf", "kp", "sc0", "sc1", "ga0", "ga1",
+               "td", "t0d", "t1d", "ct1", "mx", "pzd", "ccd", "cc1", "cc2", "lo", "lo1", "lo2", "st", "st2"]
+              + ["v%d" % r for r in range(8)] + ["xi%d" % r for r in range(8)] + ["xk%d" % r for r in range(8)])
+
+
+def rank_program(g, core, T, topo):
+    me = T.rank_of(core)
+    if me is None:
+        return
+    S = T.sem
+    V, A, P, Q = g.vector, g.scalar, g.tensor, g.sync
+    A_ = AluOpType
+    others = [r for r in range(N) if r != me]
+    offchip = [r for r in others if topo.chip(T.cores[r]) != topo.chip(core)]
+    onchip = [r for r in others if topo.chip(T.cores[r]) == topo.chip(core)]
+    dests = offchip + onchip
+    L = N - 1
+
+    def did(r):
+        rid, pid, _ = topo.addr(T.cores[r])
+        return rid, pid
+
+    def eng(r, k):
+        e = topo.engines(core, T.cores[r])[:8]
+        return 1 << e[k % len(e)]
+
+    def emask(r):
+        m = 0
+        for e in topo.engines(core, T.cores[r])[:8]:
+            m |= 1 << e
+        return m
+
+    def rows(q, h, c):
+        q.dma_start(T.xq[2 * h + c:128:4, :], T.x[64 * h + c:64 * h + 64:2, :]).then_inc(S.x2, 16)
+
+    for h, q in ((0, Q), (1, A)):
+        q.dma_start(T.xs[:, 64 * h:64 * h + 64, :], T.x[64 * h:64 * h + 64, :]).then_inc(S.x1, 16)
+    for c in range(2):
+        rows(Q, 0, c)
+        rows(A, 1, c)
+    for h in range(2):
+        Q.dma_start(T.hs[h:8:2, :], T.hc[64 * h + 8 * me:64 * h + 8 * me + 8, :]).then_inc(S.hcl, 16)
+
+    def land(r):
+        for h in range(2):
+            src = T.x[64 * h + 8 * me:64 * h + 8 * me + 8, :] if r == me else T.d1[r, 64 * h:64 * h + 64, :]
+            Q.dma_start(T.lnd[:, 32 * r + 16 * h:32 * r + 16 * h + 16], src).then_inc(S.lka if r < 2 else S.lkb, 16)
+
+    land(me)
+
+    g.iota(T.pi[:], [[0, 8]], 0, 1).then_inc(S.ipi, 1)
+    g.iota(T.jj[:], [[1, 128]], 0, -1, allow_small_or_imprecise_dtypes=True).then_inc(S.ij, 1)
+    g.iota(T.j16[0:8, :], [[1, 128]], 0, -16, allow_small_or_imprecise_dtypes=True).then_inc(S.ij16, 1)
+    g.wait_ge(S.x1, 32)
+    tr = []
+    for k, r in enumerate(dests):
+        rid, pid = did(r)
+        tr.append(RemoteDMATransfer(src=T.xs[r], dst=T.d1[me], dst_ids=[DstId(rid=rid, pnc=pid)],
+                                    dma_engine_mask=eng(r, k), remote_sem=S["xk%d" % me]))
+    g.remote_dma_fused(tr, local_sem=S.snt)
+    g.iota(T.li[:], [[1, 256]], -1, 0, allow_small_or_imprecise_dtypes=True).then_inc(S.ili, 1)
+    g.wait_ge(S.xds, 32)
+    tr = []
+    for k, r in enumerate(dests):
+        rid, pid = did(r)
+        tr.append(RemoteDMATransfer(src=T.xd[r], dst=T.d2[me], dst_ids=[DstId(rid=rid, pnc=pid)],
+                                    dma_engine_mask=eng(r, k + 5), remote_sem=S["xi%d" % me]))
+    g.remote_dma_fused(tr, local_sem=S.snt)
+    nsnt = 2 * len(dests)
+    for t, c in GF:
+        g.wait_ge(S.seed, 1)
+        g.affine_select(T["win%d" % t][:, 1024 * c:1024 * c + 1024], T.win0[:, 0:1024], [[0, 1024]], A_.is_ge, 0.0, 0, 0).then_inc(S.ifl, 1)
+    lanes = [[-8, 2], [-16, 2], [-32, 4]]
+    enals = [[8, 2], [16, 2], [32, 4]]
+    g.wait_ge(S.gz, 2)
+    g.affine_select(T.w0[:], T.on[:], lanes, A_.is_ge, 0.0, 0, 1).then_inc(S.gw, 1)
+    g.affine_select(T.w1[:], T.on[:], lanes, A_.is_ge, 8192.0, -2, 1).then_inc(S.gw, 1)
+    g.wait_ge(S.gw, 2)
+    g.affine_select(T.ee[:, :, 8:72:8], T.w0[:], enals, A_.is_ge, 0.0, 1, -1).then_inc(S.edn, 1)
+    g.affine_select(T.w2[:], T.w1[:], lanes, A_.is_ge, 0.0, 0, 1).then_inc(S.gw, 1)
+    g.wait_ge(S.gw, 3)
+    g.affine_select(T.ee[:, :, 72:136:8], T.w2[:], enals, A_.is_ge, 0.0, 3, -1).then_inc(S.edn, 1)
+    g.wait_ge(S.msk, 3)
+    g.affine_select(T.dm[:], T.m0[:], [[1, 128]], A_.not_equal, -8192.0, -64, -1).then_inc(S.ddn, 1)
+
+    nvi = [0]
+
+    def vi(ins):
+        ins.then_inc(S.vi, 1)
+        nvi[0] += 1
+
+    def vs():
+        V.wait_ge(S.vi, nvi[0])
+
+    def fill(t, c):
+        vi(V.memset(T["win%d" % t][:, 1024 * c:1024 * c + 1024], -0.5))
+
+    V.memset(T.win0[:, 0:1024], -0.5).then_inc(S.seed, 1)
+    vi(V.memset(T.mw[:], 0.0))
+    V.wait_ge(S.ipi, 1)
+    vi(V.tensor_scalar(T.p7[:], T.pi[:], 7, None, A_.bitwise_and))
+    V.wait_ge(S.ij, 1)
+    vi(V.tensor_scalar(T.m1[:], T.jj[:], 1, None, A_.is_equal))
+    V.tensor_scalar(T.m0[:], T.jj[:], 0, None, A_.is_equal).then_inc(S.msk, 1)
+    V.wait_ge(S.ij16, 1)
+    vi(V.tensor_scalar(T.cl[0:8, :], T.j16[0:8, :], 0, 15, A_.max, A_.min))
+    vs()
+    V.memset(T.m1[:, 0:128:16], 0.0).then_inc(S.msk, 1)
+    V.tensor_scalar(T.mw[:, 0:128:16], T.jj[:, 0:128:16], -15, None, A_.is_equal).then_inc(S.msk, 1)
+    V.tensor_tensor(T.sel[0:8, :], T.cl[0:8, :], T.j16[0:8, :], A_.is_equal).then_inc(S.rdy, 1)
+    V.wait_ge(S.x2, 64)
+    V.tensor_copy(T.xh[:], T.xq[:]).then_inc(S.dgh, 1)
+    V.wait_ge(S.hcl, 32)
+    V.tensor_copy(T.hsf[0:8, :], T.hs[0:8, :]).then_inc(S.rdy, 1)
+    V.wait_ge(S.dgh, 1)
+    V.tensor_tensor(T.xl[:], T.xq[:], T.xh[:], A_.subtract).then_inc(S.dgl, 1)
+    P.wait_ge(S.rdy, 2)
+    P.matmul(T.ab[:, 0:4], T.sel[0:8, :], T.hsf[0:8, :], True, True).then_inc(S.pab, 1)
+    vi(V.tensor_scalar(T.pr[:], T.p7[:], 256, None, A_.mult))
+    V.memset(T.vv[:], 0.0).then_inc(S.vz, 1)
+    V.memset(T.on[:], 1.0).then_inc(S.gz, 1)
+    V.memset(T.ee[:], 0.0).then_inc(S.gz, 1)
+    V.memset(T.gg[:, :, 0:192], -0.5).then_inc(S.gz, 1)
+    vi(V.memset(T.xf[:, :, 0:16], 0.0))
+    vs()
+    V.wait_ge(S.ili, 1)
+    V.tensor_scalar(T.rb[:], T.li[:], 0, T.pr[:, 0:1], A_.mult, A_.add).then_inc(S.rbd, 1)
+    for t, c in VF[:NF]:
+        fill(t, c)
+    V.wait_ge(S.cst, 6)
+    for s in range(2):
+        V.tensor_tensor(T.mm[:, s, :], T.ta[:, s, :], T.tb[:, s, :], A_.add).then_inc(S.mats, 1)
+
+    def afill(t, c):
+        A.activation(T["win%d" % t][:, 1024 * c:1024 * c + 1024], T.win0[:, 0:1024], COPY).then_inc(S.sfl, 1)
+
+    A.wait_ge(S.seed, 1)
+    for t, c in AF[:NA]:
+        afill(t, c)
+    A.wait_ge(S.pab, 1)
+    A.activation(T.abf[:], T.ab[:, 0:4], COPY).then_inc(S.abd, 1)
+    A.wait_ge(S.msk, 3)
+    A.wait_ge(S.abd, 1)
+    for s in range(2):
+        A.activation(T.ta[:, s, :], T.m1[:], COPY, scale=T.abf[:, 2 * s:2 * s + 1]).then_inc(S.cst, 1)
+        A.activation(T.tb[:, s, :], T.m0[:], COPY, scale=T.abf[:, 2 * s + 1:2 * s + 2]).then_inc(S.cst, 1)
+        A.activation(T.ww[:, s, :], T.mw[:], COPY, scale=T.abf[:, 2 * s:2 * s + 1]).then_inc(S.cst, 1)
+    for t, c in AF[NA:]:
+        afill(t, c)
+    Q.wait_ge(S.seed, 1)
+    for t, c in DF:
+        Q.dma_start(T["win%d" % t][:, 1024 * c:1024 * c + 1024], T.win0[:, 0:1024]).then_inc(S.fdm, 16)
+
+    PARTS = ((0, 2), (2, 8))
+    P.wait_ge(S.mats, 2)
+    P.wait_ge(S.cst, 6)
+    for part, (r0, r1) in enumerate(PARTS):
+        c0, c1 = 16 * r0, 16 * r1
+        for s in range(2):
+            P.wait_ge(S.xf, 2 * part + s + 1)
+            P.matmul(T.ps[:, s, c0:c1], T.mm[:, s, :], T.xf[:, s, 16 + c0:16 + c1], True, False)
+            m = P.matmul(T.ps[:, s, c0:c1], T.ww[:, s, :], T.xf[:, s, 15 + c0:15 + c1], False, True)
+        m.then_inc(S.kp, 1)
+
+    def flip(part):
+        r0, r1 = PARTS[part]
+        vi(V.transpose(T.tt[:, r0:r1, :, :], T.lnd[:, 32 * r0:32 * r1]))
+
+    def tokens(part, s):
+        r0, r1 = PARTS[part]
+        V.tensor_copy(T.xf[:, s, 16 + 16 * r0:16 + 16 * r1], T.tt[:, r0:r1, s, :]).then_inc(S.xf, 1)
+
+    def whole(part):
+        r0, r1 = PARTS[part]
+        V.wait_ge(S.kp, part + 1)
+        vi(V.tensor_copy(T.ki[:, :, 2 * r0:2 * r1, :], T.ps[:, :, 16 * r0:16 * r1]))
+
+    def key(part):
+        r0, r1 = PARTS[part]
+        vs()
+        vi(V.tensor_scalar(T.kj[:, :, 2 * r0:2 * r1, :], T.ki[:, :, 2 * r0:2 * r1, :], 9, H - 1, A_.logical_shift_right, A_.bitwise_and))
+
+    def lists(part):
+        c0, c1 = 2 * PARTS[part][0], 2 * PARTS[part][1]
+        even, odd = T.kj[:, :, c0:c1, 0:4], T.kj[:, :, c0:c1, 4:8]
+        vs()
+        V.tensor_copy(T.ll[:, :, c0:c1, 8:12], even).then_inc(S.gl, 1)
+        V.tensor_scalar(T.ll[:, :, c0:c1, 12:16], odd, H, None, A_.add).then_inc(S.gl, 1)
+        V.tensor_copy(T.ll[:, :, c0 + 1:c1 + 1, 0:4], odd).then_inc(S.gl, 1)
+        V.tensor_scalar(T.ll[:, :, c0:c1, 4:8], even, H, None, A_.add).then_inc(S.gl, 1)
+
+    V.wait_ge(S.lka, 64)
+    flip(0)
+    vs()
+    tokens(0, 0)
+    tokens(0, 1)
+    for t, c in VF[NF:]:
+        fill(t, c)
+    whole(0)
+    key(0)
+    lists(0)
+    V.wait_ge(S.sfl, len(AF))
+    if GF:
+        V.wait_ge(S.ifl, len(GF))
+    if DF:
+        V.wait_ge(S.fdm, 16 * len(DF))
+    V.wait_ge(S.pl, 32)
+    V.wait_ge(S.gl, 4)
+
+    def blk(i):
+        return (i, range(4 * i, 4 * i + 4), 64) if i < L else (L, range(2 * i + 14, 2 * i + 16), 32)
+
+    def t1(i):
+        return (T.qa, T.qb)[i % 2][:, 0:64] if i < L else (T.u1, T.u2)[i - L][:, 0:32]
+
+    def t0(i):
+        return (T.qa, T.qb)[i % 2][:, 64:128] if i < L else (T.u0, T.qb)[i - L][:, 0:32]
+
+    def vmax(i):
+        w = blk(i)[2]
+        if i >= 2:
+            V.wait_ge(S.pzd, i - 1)
+        V.wait_ge(S.ct1, i + 1)
+        if i >= L:
+            V.wait_ge(S.t0d, i - L + 1)
+        V.tensor_tensor(T.cm[:, i % 2, 0:w], T.c1[:, i % 2, 0:w], t0(i), A_.max).then_inc(S.mx, 1)
+
+    for k in range(NK):
+        n = 128 if k < NK - 1 else 64
+        for s in range(2):
+            if s == 0 and (k == 0 or (k % 2 == 1 and k < NK - 1)):
+                V.wait_ge(S["v%d" % ((k + 1) // 2)], 32)
+            if k:
+                V.wait_ge(S["ga%d" % s], k)
+            if (k, s) == (4, 0):
+                V.wait_ge(S.gl, 8)
+            V.tensor_copy(T["win%d" % s][:].indirect(T.ll[:, s, k, 8:8 + n // 16]),
+                          T.vv[:, 128 * k + 1:128 * k + 1 + n]).then_inc(S["sc%d" % s], 1)
+            if (k, s) == (0, 1):
+                V.wait_ge(S.lkb, 192)
+                flip(1)
+            if (k, s) == (1, 0):
+                vs()
+                tokens(1, 0)
+                tokens(1, 1)
+            if (k, s) == (2, 0):
+                whole(1)
+                key(1)
+            if (k, s) == (2, 1):
+                lists(1)
+        if k >= 3 and k % 2 == 1:
+            vmax((k - 3) // 2)
+    vmax(7)
+    vmax(8)
+    V.wait_ge(S.pzd, 9)
+    V.tensor_copy(T.cs2[:], T.pz[:, 0:32]).then_inc(S.cc2, 1)
+
+    def copy1(i):
+        w = blk(i)[2]
+        if i < L:
+            A.wait_ge(S.td, i + 1)
+        else:
+            A.wait_ge(S.t1d, i - L + 1)
+        if i >= 2:
+            A.wait_ge(S.mx, i - 1)
+        A.activation(T.c1[:, i % 2, 0:w], t1(i), COPY).then_inc(S.ct1, 1)
+
+    def final(i):
+        z = (T.pz, T.ab)[i % 2]
+        A.wait_ge(S.pzd, i + 1)
+        if i < L:
+            A.activation(T.cs[:, i, :], z[:, 0:64], COPY).then_inc(S.ccd, 1)
+        else:
+            A.activation(T.cs1[:], z[:, 0:32], COPY).then_inc(S.cc1, 1)
+
+    for k in range(NK):
+        n = 256 if k < NK - 1 else 64
+        for s in range(2):
+            A.wait_ge(S["sc%d" % s], k + 1)
+            if s == 0 and k in (0, 3):
+                A.wait_ge(S.gl, 4 if k == 0 else 8)
+            A.activation(T.gg[:, s, 256 * k + 192:256 * k + 192 + n],
+                         T["win%d" % s][:].indirect(T.ll[:, s, k + 1, 0:n // 16]), COPY).then_inc(S["ga%d" % s], 1)
+            if s == 0 and k >= 4 and k % 2 == 0:
+                final((k - 4) // 2)
+        if k >= 2 and k % 2 == 0:
+            copy1((k - 2) // 2)
+        if k == NK - 2:
+            copy1(7)
+    copy1(8)
+    final(6)
+    final(7)
+    P.wait_ge(S.edn, 2)
+    P.wait_ge(S.gz, 3)
+    seen = [0, 0]
+
+    def got(s, k):
+        if k + 1 > seen[s]:
+            P.wait_ge(S["ga%d" % s], k + 1)
+            seen[s] = k + 1
+
+    def pk(i):
+        out = (T.qa, T.qb)[i % 2][:, 0:128]
+        if i >= 2:
+            P.wait_ge(S.mx, i - 1)
+        for j in range(4):
+            for s in range(2):
+                v = 4 * i + j
+                got(s, (v - 1) // 2)
+                sh = 4 * s + j
+                m = P.matmul(out, T.ee[:, s, 8 - sh:136 - sh], T.gg[:, s, 128 * v:128 * v + 128], j + s == 0, j + s == 4)
+        m.then_inc(S.td, 1)
+
+    def half(i, t, vs_, first, last):
+        out = (t0, t1)[t](i)
+        todo = [(v, s, e) for v in vs_ for s in range(2) for e in range(2)]
+        for j, (v, s, e) in enumerate(todo):
+            got(s, (v - 2) // 2 if v % 2 == 0 else (v - 1) // 2 - t)
+            sh = 4 * s + (v - blk(i)[1][0]) * 2 + e
+            b = 128 * v + 64 * (1 - t) + 32 * e
+            m = P.matmul(out, T.ee[:, s, 8 - sh:136 - sh], T.gg[:, s, b:b + 32], first and j == 0, last and j == len(todo) - 1)
+        if last:
+            m.then_inc(S.t1d if t else S.t0d, 1)
+
+    def decode(i):
+        w = blk(i)[2]
+        if i == 0:
+            P.wait_ge(S.ddn, 1)
+        P.wait_ge(S.mx, i + 1)
+        if i >= 2:
+            P.wait_ge(S.ccd, i - 1)
+        P.matmul((T.pz, T.ab)[i % 2][:, 0:w], T.dm[:], T.cm[:, i % 2, 0:w], True, True).then_inc(S.pzd, 1)
+
+    for i in range(L - 1):
+        pk(i)
+        decode(i)
+    pk(6)
+    half(7, 1, [28, 29], True, True)
+    half(7, 0, [28], True, False)
+    half(7, 0, [29], False, True)
+    half(8, 1, [30, 31], True, True)
+    decode(6)
+    half(8, 0, [30], True, False)
+    decode(7)
+    half(8, 0, [31], False, True)
+    decode(8)
+
+    def send(r, dst, src_, sem):
+        rid, pid = did(r)
+        g.remote_dma(out_ap=dst, in_ap=src_, remote_sem=sem, local_sem=S.snt, pid=pid, routing_id=rid, dma_engine_mask=emask(r))
+        return 8
+
+    for r in range(L):
+        g.wait_ge(S.ccd, r + 1)
+        if r != me:
+            nsnt += send(r, T.dy[me], T.cs[:, r, :], S.rin)
+    g.wait_ge(S.cc1, 1)
+    if me != L:
+        nsnt += send(L, T.dy1[me], T.cs1[:], S.rin1)
+    g.wait_ge(S.cc2, 1)
+    if me != L:
+        nsnt += send(L, T.dy2[me], T.cs2[:], S.rin2)
+    Q.wait_ge(S.dgh, 1)
+    Q.dma_start(T.xd[:, 0:64, :], T.xh[:]).then_inc(S.xds, 16)
+    Q.wait_ge(S.dgl, 1)
+    Q.dma_start(T.xd[:, 64:128, :], T.xl[:]).then_inc(S.xds, 16)
+
+    def landed(rs):
+        for r in rs:
+            if r != me:
+                Q.wait_ge(S["xk%d" % r], 1)
+                land(r)
+
+    landed(range(2))
+    Q.wait_ge(S.vz, 1)
+    Q.wait_ge(S.ili, 1)
+    Q.dma_start(T.vv[0:128:8, :], T.li[:]).then_inc(S.pl, 16)
+    Q.wait_ge(S.rbd, 1)
+    Q.dma_start(T.vv[1:128:8, :], T.rb[:]).then_inc(S.pl, 16)
+    for r in range(N):
+        if r == 2:
+            landed(range(2, N))
+        if r != me:
+            Q.wait_ge(S["xi%d" % r], 1)
+        for e, own in enumerate((T.xh, T.xl)):
+            part = own[16 * me:16 * me + 16, :] if r == me else T.d2[r, 64 * e:64 * e + 64, :]
+            Q.dma_start(T.vv[2 + e:128:8, 256 * r:256 * r + 256], part).then_inc(S["v%d" % r], 16)
+    outs = (T.y, T.z)
+    if me != L:
+        Q.wait_ge(S.ccd, me + 1)
+        Q.dma_start(T.dy[me], T.cs[:, me, :]).then_inc(S.lo, 16)
+        for k, q, sem in ((0, Q, S.st), (1, A, S.st2)):
+            q.wait_ge(S.lo, 16)
+            q.wait_ge(S.rin, 8 * len(dests))
+            for h in range(2):
+                q.dma_start(outs[k][64 * h:64 * h + 64, :], T.dy[:, 64 * k + 32 * h:64 * k + 32 * h + 32, :]).then_inc(sem, 16)
+            q.wait_ge(sem, 32)
+    else:
+        Q.wait_ge(S.cc1, 1)
+        Q.dma_start(T.dy1[me], T.cs1[:]).then_inc(S.lo1, 16)
+        Q.wait_ge(S.cc2, 1)
+        Q.dma_start(T.dy2[me], T.cs2[:]).then_inc(S.lo2, 16)
+        for k, q, sem in ((0, Q, S.st), (1, A, S.st2)):
+            done = 0
+            for b, d, lo, rin in ((0, T.dy1, S.lo1, S.rin1), (128, T.dy2, S.lo2, S.rin2)):
+                q.wait_ge(lo, 16)
+                q.wait_ge(rin, 8 * len(dests))
+                for h in range(2):
+                    q.dma_start(outs[k][64 * h:64 * h + 64, b:b + 128], d[:, 64 * k + 32 * h:64 * k + 32 * h + 32, :]).then_inc(sem, 16)
+                    done += 16
+            q.wait_ge(sem, done)
+    g.wait_ge(S.snt, nsnt)

@@ -4,11 +4,14 @@ from concourse.mybir import AluOpType, ActivationFunctionType
 N, T_, R, H = 8, 256, 64, 4096
 NU = N * T_ // R
 NK = NU // 2
-COPY = ActivationFunctionType.Copy
+COPY, RELU = ActivationFunctionType.Copy, ActivationFunctionType.Relu
 BF = "bfloat16"
-REST = [(t, c) for t in range(2) for c in range(8)][1:]
-NV, NF, NS, NA, NG = 5, 3, 7, 2, 1
-VF, AF, GF, DF = REST[:NV], REST[NV:NV + NS], REST[NV + NS:NV + NS + NG], REST[NV + NS + NG:]
+SEED, VA, VB, VC = 1024, 512, 5376, 1024
+DA, DB = 2048, 0
+AF = 4 * H - SEED - VA - VB - VC - DA - DB
+LATER = (((0, 1), (1, 0), (1, 1), (1, 1), (2, 0), (2, 1)), ((3, 1), (4, 0), (4, 1), (5, 1), (6, 0), (6, 1)))
+PARTS = ((0, 2), (2, 4), (4, 8))
+FIN = 4
 
 SCRATCH = {
     "xs": ("dram", [8, 128, 32], "int32"),
@@ -16,52 +19,39 @@ SCRATCH = {
     "xd": ("dram", [8, 128, 64], BF),
     "d2": ("dram", [8, 128, 64], BF),
     "dy": ("dram", [8, 128, 64], "float32"),
-    "dy1": ("dram", [8, 128, 32], "float32"),
-    "dy2": ("dram", [8, 128, 32], "float32"),
     "xq": ("sbuf", [128, 256], "int32"),
-    "xh": ("sbuf", [128, 256], BF), "xl": ("sbuf", [128, 256], BF),
+    "xp": ("sbuf", [128, 2, 256], BF),
     "lnd": ("sbuf", [128, 256], "int32"),
     "tt": ("sbuf", [128, 8, 2, 16], "int32"),
-    "xf": ("sbuf", [128, 2, 144], "float32"),
-    "jj": ("sbuf", [128, 128], "float32"),
-    "j16": ("sbuf", [128, 128], "float32"),
-    "cl": ("sbuf", [128, 128], "float32"),
+    "xa": ("sbuf", [128, 2, 144], "float32"), "xb": ("sbuf", [128, 2, 128], "float32"),
+    "one": ("sbuf", [128, 256], BF),
     "sel": ("sbuf", [128, 128], "float32"),
     "hs": ("sbuf", [128, 4], "int32"),
     "hsf": ("sbuf", [128, 4], "float32"),
-    "abf": ("sbuf", [128, 4], "float32"),
     "m0": ("sbuf", [128, 128], "float32"),
-    "m1": ("sbuf", [128, 128], "float32"),
+    "m1": ("sbuf", [128, 8, 16], "float32"),
     "mw": ("sbuf", [128, 128], "float32"),
-    "ta": ("sbuf", [128, 2, 128], "float32"),
-    "tb": ("sbuf", [128, 2, 128], "float32"),
-    "mm": ("sbuf", [128, 2, 128], "float32"),
-    "ww": ("sbuf", [128, 2, 128], "float32"),
     "dm": ("sbuf", [128, 128], "float32"),
-    "pi": ("sbuf", [128, 8], "int32"), "p7": ("sbuf", [128, 8], "int32"), "pr": ("sbuf", [128, 8], "float32"),
+    "pi": ("sbuf", [128, 32], BF), "pr": ("sbuf", [128, 32], BF),
     "li": ("sbuf", [128, 256], BF), "rb": ("sbuf", [128, 256], BF),
-    "on": ("sbuf", [128, 2, 8], BF), "w0": ("sbuf", [128, 2, 8], BF),
-    "w1": ("sbuf", [128, 2, 8], BF), "w2": ("sbuf", [128, 2, 8], BF),
     "ee": ("sbuf", [128, 2, 144], BF),
+    "no": ("sbuf", [128, 64], BF),
     "vv": ("sbuf", [128, 2048], BF),
     "ki": ("sbuf", [128, 2, 16, 8], "int32"), "kj": ("sbuf", [128, 2, 16, 8], "int32"),
     "ll": ("sbuf", [128, 2, 17, 16], "uint16"),
     "win0": ("sbuf", [128, 2 * H], BF), "win1": ("sbuf", [128, 2 * H], BF),
     "gg": ("sbuf", [128, 2, 4096], BF),
-    "c1": ("sbuf", [128, 2, 64], "float32"),
-    "cm": ("sbuf", [128, 2, 64], "float32"),
+    "c1": ("sbuf", [128, 8, 64], "float32"), "cm": ("sbuf", [128, 8, 64], "float32"),
+    "za": ("psum", [128, 512], "float32"), "zb": ("psum", [128, 512], "float32"),
     "cs": ("sbuf", [128, 8, 64], "float32"),
-    "cs1": ("sbuf", [128, 32], "float32"),
-    "cs2": ("sbuf", [128, 32], "float32"),
-    "ab": ("psum", [128, 512], "float32"), "pz": ("psum", [128, 512], "float32"),
-    "ps": ("psum", [128, 2, 256], "float32"),
+    "ab": ("psum", [128, 512], "float32"), "ps": ("psum", [128, 512], "float32"),
     "qa": ("psum", [128, 512], "float32"), "qb": ("psum", [128, 512], "float32"),
-    "u0": ("psum", [128, 512], "float32"), "u1": ("psum", [128, 512], "float32"), "u2": ("psum", [128, 512], "float32"),
+    "ua": ("psum", [128, 512], "float32"), "ub": ("psum", [128, 512], "float32"),
 }
-SEMAPHORES = (["x1", "x2", "hcl", "lka", "lkb", "snt", "rin", "rin1", "rin2",
-               "ij", "ipi", "ij16", "ili", "gw", "gl", "ifl", "fdm", "vi", "seed", "rdy", "pab", "abd", "msk", "cst", "mats",
-               "edn", "ddn", "sfl", "gz", "dgh", "dgl", "xds", "vz", "rbd", "pl", "xf", "kp", "sc0", "sc1", "ga0", "ga1",
-               "td", "t0d", "t1d", "ct1", "mx", "pzd", "ccd", "cc1", "cc2", "lo", "lo1", "lo2", "st", "st2"]
+SEMAPHORES = (["x1", "x2", "hcl", "lk0", "lk1", "lk2", "pl1", "snt", "rin",
+               "ipi", "ili", "half", "gw", "gl", "gm", "vi", "vf", "seed", "ones", "rdy", "pab", "msk", "nod",
+               "ddn", "idn", "sfl", "dgh", "dgl", "xds", "rbd", "pl", "pl2", "xf", "kp", "sc0", "sc1", "ga0", "ga1",
+               "t0d", "t1d", "ct1", "c17", "mx", "cy7", "pzd", "ccd", "cc7", "lo", "st", "st2"]
               + ["v%d" % r for r in range(8)] + ["xi%d" % r for r in range(8)] + ["xk%d" % r for r in range(8)])
 
 
@@ -92,6 +82,12 @@ def rank_program(g, core, T, topo):
             m |= 1 << e
         return m
 
+    def pieces(c0, c1, most):
+        while c0 < c1:
+            c = min(c1, c0 + most, (c0 // (2 * H) + 1) * 2 * H)
+            yield T["win%d" % (1 - c0 // (2 * H))][:, c0 % (2 * H):(c - 1) % (2 * H) + 1], c - c0
+            c0 = c
+
     def rows(q, h, c):
         q.dma_start(T.xq[2 * h + c:128:4, :], T.x[64 * h + c:64 * h + 64:2, :]).then_inc(S.x2, 16)
 
@@ -106,46 +102,55 @@ def rank_program(g, core, T, topo):
     def land(r):
         for h in range(2):
             src = T.x[64 * h + 8 * me:64 * h + 8 * me + 8, :] if r == me else T.d1[r, 64 * h:64 * h + 64, :]
-            Q.dma_start(T.lnd[:, 32 * r + 16 * h:32 * r + 16 * h + 16], src).then_inc(S.lka if r < 2 else S.lkb, 16)
+            Q.dma_start(T.lnd[:, 32 * r + 16 * h:32 * r + 16 * h + 16], src).then_inc(S["lk%d" % [r0 <= r < r1 for r0, r1 in PARTS].index(True)], 16)
 
-    land(me)
+    g.iota(T.pi[:], [[0, 16], [256, 2]], 0, 16, allow_small_or_imprecise_dtypes=True).then_inc(S.ipi, 1)
+    g.wait_ge(S.ones, 1)
+    g.affine_select(T.m1[:, :, 1:16], T.one[:, 0:120], [[16, 8], [1, 15]], A_.is_equal, 0.0, 0, -1).then_inc(S.msk, 1)
+    g.affine_select(T.m1[:, :, 0], T.one[:, 0:8], [[0, 8]], A_.is_gt, 0.0, 0, 0).then_inc(S.msk, 1)
 
-    g.iota(T.pi[:], [[0, 8]], 0, 1).then_inc(S.ipi, 1)
-    g.iota(T.jj[:], [[1, 128]], 0, -1, allow_small_or_imprecise_dtypes=True).then_inc(S.ij, 1)
-    g.iota(T.j16[0:8, :], [[1, 128]], 0, -16, allow_small_or_imprecise_dtypes=True).then_inc(S.ij16, 1)
+    def all_to_all(src, dst, sem, k0):
+        tr = []
+        for k, r in enumerate(dests):
+            rid, pid = did(r)
+            tr.append(RemoteDMATransfer(src=src[r], dst=dst[me], dst_ids=[DstId(rid=rid, pnc=pid)],
+                                        dma_engine_mask=eng(r, k + k0), remote_sem=sem))
+        g.remote_dma_fused(tr, local_sem=S.snt)
+
     g.wait_ge(S.x1, 32)
-    tr = []
-    for k, r in enumerate(dests):
-        rid, pid = did(r)
-        tr.append(RemoteDMATransfer(src=T.xs[r], dst=T.d1[me], dst_ids=[DstId(rid=rid, pnc=pid)],
-                                    dma_engine_mask=eng(r, k), remote_sem=S["xk%d" % me]))
-    g.remote_dma_fused(tr, local_sem=S.snt)
-    g.iota(T.li[:], [[1, 256]], -1, 0, allow_small_or_imprecise_dtypes=True).then_inc(S.ili, 1)
-    g.wait_ge(S.xds, 32)
-    tr = []
-    for k, r in enumerate(dests):
-        rid, pid = did(r)
-        tr.append(RemoteDMATransfer(src=T.xd[r], dst=T.d2[me], dst_ids=[DstId(rid=rid, pnc=pid)],
-                                    dma_engine_mask=eng(r, k + 5), remote_sem=S["xi%d" % me]))
-    g.remote_dma_fused(tr, local_sem=S.snt)
-    nsnt = 2 * len(dests)
-    for t, c in GF:
-        g.wait_ge(S.seed, 1)
-        g.affine_select(T["win%d" % t][:, 1024 * c:1024 * c + 1024], T.win0[:, 0:1024], [[0, 1024]], A_.is_ge, 0.0, 0, 0).then_inc(S.ifl, 1)
-    lanes = [[-8, 2], [-16, 2], [-32, 4]]
-    enals = [[8, 2], [16, 2], [32, 4]]
-    g.wait_ge(S.gz, 2)
-    g.affine_select(T.w0[:], T.on[:], lanes, A_.is_ge, 0.0, 0, 1).then_inc(S.gw, 1)
-    g.affine_select(T.w1[:], T.on[:], lanes, A_.is_ge, 8192.0, -2, 1).then_inc(S.gw, 1)
-    g.wait_ge(S.gw, 2)
-    g.affine_select(T.ee[:, :, 8:72:8], T.w0[:], enals, A_.is_ge, 0.0, 1, -1).then_inc(S.edn, 1)
-    g.affine_select(T.w2[:], T.w1[:], lanes, A_.is_ge, 0.0, 0, 1).then_inc(S.gw, 1)
-    g.wait_ge(S.gw, 3)
-    g.affine_select(T.ee[:, :, 72:136:8], T.w2[:], enals, A_.is_ge, 0.0, 3, -1).then_inc(S.edn, 1)
-    g.wait_ge(S.msk, 3)
-    g.affine_select(T.dm[:], T.m0[:], [[1, 128]], A_.not_equal, -8192.0, -64, -1).then_inc(S.ddn, 1)
+    all_to_all(T.xs, T.d1, S["xk%d" % me], 0)
 
-    nvi = [0]
+    def parts_out():
+        g.wait_ge(S.xds, 16)
+        all_to_all(T.xd, T.d2, S["xi%d" % me], 5)
+
+    g.affine_select(T.sel[0:8, :], T.one[0:8, 0:128], [[1, 8], [0, 16]], A_.is_equal, 0.0, 0, -1).then_inc(S.rdy, 1)
+    if me < 2:
+        parts_out()
+    g.affine_select(T.mw[:], T.one[:, 0:128], [[16, 8], [1000, 16]], A_.is_equal, 0.0, 15, -1).then_inc(S.msk, 1)
+    g.affine_select(T.xa[:, :, 15], T.one[:, 0:2], [[0, 2]], A_.is_gt, 0.0, 0, 0).then_inc(S.msk, 1)
+    nsnt = 2 * len(dests)
+    lanes = [[-8, 2], [-16, 2], [-32, 4]]
+    g.iota(T.ee[:], [[0, 288]], 0, 0, allow_small_or_imprecise_dtypes=True).then_inc(S.gw, 1)
+    g.wait_ge(S.ili, 1)
+    g.affine_select(T.no[:], T.li[:, 0:64], [[0, 64]], A_.is_gt, -0.5, 0, 0).then_inc(S.nod, 1)
+    if me >= 2:
+        g.wait_ge(S.lk0, 64)
+        parts_out()
+    yp, ps = (T.ee[:, :, 8:72:8], T.ee[:, :, 72:136:8]), (T.ee[:, :, 72:136:8],)
+    ngw = 1
+    for rnd in ([(yp, 0, 8192)], [(yp, 4, 8192)], [(ps, 2, 1)], [(ps, 6, 1)]):
+        g.wait_ge(S.gw, ngw)
+        for to, lane, w in rnd:
+            for half in to:
+                g.affine_select(half, half, lanes, A_.not_equal, float(w), -lane, 1).then_inc(S.gw, 1)
+                ngw += 1
+    g.affine_select(T.m0[:], T.one[:, 0:128], [[1, 128]], A_.is_equal, 0.0, 0, -1).then_inc(S.idn, 1)
+    g.wait_ge(S.idn, 1)
+    g.affine_select(T.dm[:, 0:64], T.m0[:, 0:64], [[1, 64]], A_.not_equal, 1.0 / 8192, 0, -1).then_inc(S.ddn, 1)
+    g.affine_select(T.dm[:, 64:128], T.m0[:, 64:128], [[1, 64]], A_.not_equal, -1.0, 0, -1).then_inc(S.ddn, 1)
+
+    nvi, nvf = [0], [0]
 
     def vi(ins):
         ins.then_inc(S.vi, 1)
@@ -154,88 +159,72 @@ def rank_program(g, core, T, topo):
     def vs():
         V.wait_ge(S.vi, nvi[0])
 
-    def fill(t, c):
-        vi(V.memset(T["win%d" % t][:, 1024 * c:1024 * c + 1024], -0.5))
+    def fill(c0, n):
+        c0 += SEED + AF
+        for w, _ in pieces(c0, c0 + n, 2 * H):
+            V.memset(w, -0.5).then_inc(S.vf, 1)
+            nvf[0] += 1
 
-    V.memset(T.win0[:, 0:1024], -0.5).then_inc(S.seed, 1)
-    vi(V.memset(T.mw[:], 0.0))
+    V.memset(T.one[:], 1.0).then_inc(S.ones, 1)
+    V.memset(T.win1[:, 0:SEED // 2], -0.5).then_inc(S.half, 1)
+    V.memset(T.win1[:, SEED // 2:SEED], -0.5).then_inc(S.seed, 1)
     V.wait_ge(S.ipi, 1)
-    vi(V.tensor_scalar(T.p7[:], T.pi[:], 7, None, A_.bitwise_and))
-    V.wait_ge(S.ij, 1)
-    vi(V.tensor_scalar(T.m1[:], T.jj[:], 1, None, A_.is_equal))
-    V.tensor_scalar(T.m0[:], T.jj[:], 0, None, A_.is_equal).then_inc(S.msk, 1)
-    V.wait_ge(S.ij16, 1)
-    vi(V.tensor_scalar(T.cl[0:8, :], T.j16[0:8, :], 0, 15, A_.max, A_.min))
+    vi(V.transpose(T.pr[:], T.pi[:]))
+    V.wait_ge(S.ones, 1)
+    V.tensor_tensor_scan(T.li[:], T.one[:], T.one[:], -2, A_.mult, A_.add).then_inc(S.ili, 1)
+    V.wait_ge(S.half, 1)
     vs()
-    V.memset(T.m1[:, 0:128:16], 0.0).then_inc(S.msk, 1)
-    V.tensor_scalar(T.mw[:, 0:128:16], T.jj[:, 0:128:16], -15, None, A_.is_equal).then_inc(S.msk, 1)
-    V.tensor_tensor(T.sel[0:8, :], T.cl[0:8, :], T.j16[0:8, :], A_.is_equal).then_inc(S.rdy, 1)
+    V.tensor_scalar(T.rb[:], T.win1[:, 0:256], 0, T.pr[:, 0:1], A_.mult, A_.add).then_inc(S.rbd, 1)
+    fill(0, VA)
     V.wait_ge(S.x2, 64)
-    V.tensor_copy(T.xh[:], T.xq[:]).then_inc(S.dgh, 1)
+    V.tensor_copy(T.xp[:, 0, :], T.xq[:]).then_inc(S.dgh, 1)
     V.wait_ge(S.hcl, 32)
     V.tensor_copy(T.hsf[0:8, :], T.hs[0:8, :]).then_inc(S.rdy, 1)
     V.wait_ge(S.dgh, 1)
-    V.tensor_tensor(T.xl[:], T.xq[:], T.xh[:], A_.subtract).then_inc(S.dgl, 1)
+    V.tensor_tensor(T.xp[:, 1, :], T.xq[:], T.xp[:, 0, :], A_.subtract).then_inc(S.dgl, 1)
+    fill(VA, VB)
     P.wait_ge(S.rdy, 2)
     P.matmul(T.ab[:, 0:4], T.sel[0:8, :], T.hsf[0:8, :], True, True).then_inc(S.pab, 1)
-    vi(V.tensor_scalar(T.pr[:], T.p7[:], 256, None, A_.mult))
-    V.memset(T.vv[:], 0.0).then_inc(S.vz, 1)
-    V.memset(T.on[:], 1.0).then_inc(S.gz, 1)
-    V.memset(T.ee[:], 0.0).then_inc(S.gz, 1)
-    V.memset(T.gg[:, :, 0:192], -0.5).then_inc(S.gz, 1)
-    vi(V.memset(T.xf[:, :, 0:16], 0.0))
-    vs()
-    V.wait_ge(S.ili, 1)
-    V.tensor_scalar(T.rb[:], T.li[:], 0, T.pr[:, 0:1], A_.mult, A_.add).then_inc(S.rbd, 1)
-    for t, c in VF[:NF]:
-        fill(t, c)
-    V.wait_ge(S.cst, 6)
-    for s in range(2):
-        V.tensor_tensor(T.mm[:, s, :], T.ta[:, s, :], T.tb[:, s, :], A_.add).then_inc(S.mats, 1)
-
-    def afill(t, c):
-        A.activation(T["win%d" % t][:, 1024 * c:1024 * c + 1024], T.win0[:, 0:1024], COPY).then_inc(S.sfl, 1)
-
+    A.wait_ge(S.half, 1)
+    A.activation(T.win1[:, SEED:SEED + SEED // 2], T.win1[:, 0:SEED // 2], COPY).then_inc(S.sfl, 1)
     A.wait_ge(S.seed, 1)
-    for t, c in AF[:NA]:
-        afill(t, c)
-    A.wait_ge(S.pab, 1)
-    A.activation(T.abf[:], T.ab[:, 0:4], COPY).then_inc(S.abd, 1)
-    A.wait_ge(S.msk, 3)
-    A.wait_ge(S.abd, 1)
-    for s in range(2):
-        A.activation(T.ta[:, s, :], T.m1[:], COPY, scale=T.abf[:, 2 * s:2 * s + 1]).then_inc(S.cst, 1)
-        A.activation(T.tb[:, s, :], T.m0[:], COPY, scale=T.abf[:, 2 * s + 1:2 * s + 2]).then_inc(S.cst, 1)
-        A.activation(T.ww[:, s, :], T.mw[:], COPY, scale=T.abf[:, 2 * s:2 * s + 1]).then_inc(S.cst, 1)
-    for t, c in AF[NA:]:
-        afill(t, c)
-    Q.wait_ge(S.seed, 1)
-    for t, c in DF:
-        Q.dma_start(T["win%d" % t][:, 1024 * c:1024 * c + 1024], T.win0[:, 0:1024]).then_inc(S.fdm, 16)
+    nsf = 1
+    for w, n in pieces(SEED + SEED // 2, SEED + AF, SEED):
+        A.activation(w, T.win1[:, 0:n], COPY).then_inc(S.sfl, 1)
+        nsf += 1
 
-    PARTS = ((0, 2), (2, 8))
-    P.wait_ge(S.mats, 2)
-    P.wait_ge(S.cst, 6)
-    for part, (r0, r1) in enumerate(PARTS):
-        c0, c1 = 16 * r0, 16 * r1
-        for s in range(2):
-            P.wait_ge(S.xf, 2 * part + s + 1)
-            P.matmul(T.ps[:, s, c0:c1], T.mm[:, s, :], T.xf[:, s, 16 + c0:16 + c1], True, False)
-            m = P.matmul(T.ps[:, s, c0:c1], T.ww[:, s, :], T.xf[:, s, 15 + c0:15 + c1], False, True)
-        m.then_inc(S.kp, 1)
+    P.wait_ge(S.msk, 4)
+
+    def shift(part):
+        c0, c1 = 16 * PARTS[part][0], 16 * PARTS[part][1]
+        P.wait_ge(S.xf, 2 * part + 2)
+        P.matmul(T.ps[:, 2 * c0:2 * c1], T.m1[:], T.xa[:, :, 16 + c0:16 + c1], True, False)
+        P.matmul(T.ps[:, 2 * c0:2 * c1], T.mw[:], T.xa[:, :, 15 + c0:15 + c1], False, True).then_inc(S.kp, 1)
+
+    shift(0)
+    shift(1)
 
     def flip(part):
         r0, r1 = PARTS[part]
+        V.wait_ge(S["lk%d" % part], 32 * (r1 - r0))
         vi(V.transpose(T.tt[:, r0:r1, :, :], T.lnd[:, 32 * r0:32 * r1]))
 
-    def tokens(part, s):
+    def times_a(part):
         r0, r1 = PARTS[part]
-        V.tensor_copy(T.xf[:, s, 16 + 16 * r0:16 + 16 * r1], T.tt[:, r0:r1, s, :]).then_inc(S.xf, 1)
+        vs()
+        for s in range(2):
+            V.tensor_scalar(T.xa[:, s, 16 + 16 * r0:16 + 16 * r1], T.tt[:, r0:r1, s, :], T.ab[:, 2 * s:2 * s + 1], None, A_.mult).then_inc(S.xf, 1)
+
+    def times_b(part):
+        r0, r1 = PARTS[part]
+        for s in range(2):
+            vi(V.tensor_scalar(T.xb[:, s, 16 * r0:16 * r1], T.tt[:, r0:r1, s, :], T.ab[:, 2 * s + 1:2 * s + 2], None, A_.mult))
 
     def whole(part):
         r0, r1 = PARTS[part]
+        vs()
         V.wait_ge(S.kp, part + 1)
-        vi(V.tensor_copy(T.ki[:, :, 2 * r0:2 * r1, :], T.ps[:, :, 16 * r0:16 * r1]))
+        vi(V.tensor_tensor(T.ki[:, :, 2 * r0:2 * r1, :], T.ps[:, 32 * r0:32 * r1], T.xb[:, :, 16 * r0:16 * r1], A_.add))
 
     def key(part):
         r0, r1 = PARTS[part]
@@ -248,227 +237,176 @@ def rank_program(g, core, T, topo):
         vs()
         V.tensor_copy(T.ll[:, :, c0:c1, 8:12], even).then_inc(S.gl, 1)
         V.tensor_scalar(T.ll[:, :, c0:c1, 12:16], odd, H, None, A_.add).then_inc(S.gl, 1)
-        V.tensor_copy(T.ll[:, :, c0 + 1:c1 + 1, 0:4], odd).then_inc(S.gl, 1)
-        V.tensor_scalar(T.ll[:, :, c0:c1, 4:8], even, H, None, A_.add).then_inc(S.gl, 1)
+        V.tensor_copy(T.ll[:, :, c0 + 1:c1 + 1, 0:4], odd).then_inc(S.gm, 1)
+        V.tensor_scalar(T.ll[:, :, c0:c1, 4:8], even, H, None, A_.add).then_inc(S.gm, 1)
 
-    V.wait_ge(S.lka, 64)
     flip(0)
-    vs()
-    tokens(0, 0)
-    tokens(0, 1)
-    for t, c in VF[NF:]:
-        fill(t, c)
+    V.wait_ge(S.pab, 1)
+    times_a(0)
+    times_b(0)
+    fill(VA + VB, VC)
     whole(0)
     key(0)
     lists(0)
-    V.wait_ge(S.sfl, len(AF))
-    if GF:
-        V.wait_ge(S.ifl, len(GF))
-    if DF:
-        V.wait_ge(S.fdm, 16 * len(DF))
-    V.wait_ge(S.pl, 32)
-    V.wait_ge(S.gl, 4)
+    pack, out = ((T.qa, T.qb), (T.ua, T.ub)), (T.za, T.zb)
 
-    def blk(i):
-        return (i, range(4 * i, 4 * i + 4), 64) if i < L else (L, range(2 * i + 14, 2 * i + 16), 32)
+    def at_t1(i):
+        return (max(2 * i + 1, 2), 1)
 
-    def t1(i):
-        return (T.qa, T.qb)[i % 2][:, 0:64] if i < L else (T.u1, T.u2)[i - L][:, 0:32]
+    def at_max(i):
+        return (min(max(2 * i + 2, 3), NK - 1), 1)
 
-    def t0(i):
-        return (T.qa, T.qb)[i % 2][:, 64:128] if i < L else (T.u0, T.qb)[i - L][:, 0:32]
+    def at_out(i):
+        return (max(2 * i + 3, 4), 0)
 
     def vmax(i):
-        w = blk(i)[2]
-        if i >= 2:
-            V.wait_ge(S.pzd, i - 1)
-        V.wait_ge(S.ct1, i + 1)
-        if i >= L:
-            V.wait_ge(S.t0d, i - L + 1)
-        V.tensor_tensor(T.cm[:, i % 2, 0:w], T.c1[:, i % 2, 0:w], t0(i), A_.max).then_inc(S.mx, 1)
+        if i == L:
+            V.wait_ge(S.t1d, N)
+            V.tensor_copy(T.c1[:, L, :], pack[1][L % 2][:, 0:64]).then_inc(S.c17, 1)
+            V.wait_ge(S.c17, 1)
+        else:
+            V.wait_ge(S.ct1, i + 1)
+        V.wait_ge(S.t0d, i + 1)
+        V.tensor_tensor(T.cm[:, i, :], T.c1[:, i, :], pack[0][i % 2][:, 0:64], A_.max).then_inc(S.mx, 1)
+        if i >= L - 1:
+            V.wait_ge(S.mx, i + 1)
+            V.tensor_tensor(T.cs[64:128, i, :], T.cm[64:128, i, :], T.cm[0:64, i, :], A_.subtract).then_inc(S.cc7, 1)
+        if i == L - 1:
+            V.tensor_scalar(T.cs[0:64, i, :], T.cm[0:64, i, :], 1.0 / 8192, None, A_.mult).then_inc(S.cc7, 1)
 
+    V.wait_ge(S.vf, nvf[0])
+    V.wait_ge(S.pl, 16 * (3 + (DA + DB) // SEED))
+    V.wait_ge(S.gl, 2)
+    between = [(at, step, part) for part in range(1, len(PARTS)) for at, step in zip(LATER[part - 1], (flip, times_a, times_b, whole, key, lists))]
+    between += [(at_max(i), vmax, i) for i in range(N)]
     for k in range(NK):
         n = 128 if k < NK - 1 else 64
         for s in range(2):
             if s == 0 and (k == 0 or (k % 2 == 1 and k < NK - 1)):
-                V.wait_ge(S["v%d" % ((k + 1) // 2)], 32)
+                V.wait_ge(S["v%d" % ((k + 1) // 2)], 16)
+            for part, (r0, r1) in enumerate(PARTS):
+                if part and (k, s) == (2 * r0 - 1, 0):
+                    V.wait_ge(S["pl%d" % part], 16 * (1 + (r1 - r0) // 2 + (r1 - r0 + 3) // 4))
+                if part and (k, s) == (2 * r0, 0):
+                    V.wait_ge(S.gl, 2 * part + 2)
+            if (k, s) == (0, 1):
+                V.wait_ge(S.sfl, nsf)
             if k:
                 V.wait_ge(S["ga%d" % s], k)
-            if (k, s) == (4, 0):
-                V.wait_ge(S.gl, 8)
             V.tensor_copy(T["win%d" % s][:].indirect(T.ll[:, s, k, 8:8 + n // 16]),
                           T.vv[:, 128 * k + 1:128 * k + 1 + n]).then_inc(S["sc%d" % s], 1)
-            if (k, s) == (0, 1):
-                V.wait_ge(S.lkb, 192)
-                flip(1)
-            if (k, s) == (1, 0):
-                vs()
-                tokens(1, 0)
-                tokens(1, 1)
-            if (k, s) == (2, 0):
-                whole(1)
-                key(1)
-            if (k, s) == (2, 1):
-                lists(1)
-        if k >= 3 and k % 2 == 1:
-            vmax((k - 3) // 2)
-    vmax(7)
-    vmax(8)
-    V.wait_ge(S.pzd, 9)
-    V.tensor_copy(T.cs2[:], T.pz[:, 0:32]).then_inc(S.cc2, 1)
-
-    def copy1(i):
-        w = blk(i)[2]
-        if i < L:
-            A.wait_ge(S.td, i + 1)
-        else:
-            A.wait_ge(S.t1d, i - L + 1)
-        if i >= 2:
-            A.wait_ge(S.mx, i - 1)
-        A.activation(T.c1[:, i % 2, 0:w], t1(i), COPY).then_inc(S.ct1, 1)
-
-    def final(i):
-        z = (T.pz, T.ab)[i % 2]
-        A.wait_ge(S.pzd, i + 1)
-        if i < L:
-            A.activation(T.cs[:, i, :], z[:, 0:64], COPY).then_inc(S.ccd, 1)
-        else:
-            A.activation(T.cs1[:], z[:, 0:32], COPY).then_inc(S.cc1, 1)
-
+            for at, step, arg in between:
+                if at == (k, s):
+                    step(arg)
     for k in range(NK):
         n = 256 if k < NK - 1 else 64
         for s in range(2):
             A.wait_ge(S["sc%d" % s], k + 1)
-            if s == 0 and k in (0, 3):
-                A.wait_ge(S.gl, 4 if k == 0 else 8)
+            for part, (r0, r1) in enumerate(PARTS):
+                if (k, s) == (max(2 * r0 - 1, 0), 0):
+                    A.wait_ge(S.gl, 2 * part + 2)
+                    A.wait_ge(S.gm, 2 * part + 2)
             A.activation(T.gg[:, s, 256 * k + 192:256 * k + 192 + n],
                          T["win%d" % s][:].indirect(T.ll[:, s, k + 1, 0:n // 16]), COPY).then_inc(S["ga%d" % s], 1)
-            if s == 0 and k >= 4 and k % 2 == 0:
-                final((k - 4) // 2)
-        if k >= 2 and k % 2 == 0:
-            copy1((k - 2) // 2)
-        if k == NK - 2:
-            copy1(7)
-    copy1(8)
-    final(6)
-    final(7)
-    P.wait_ge(S.edn, 2)
-    P.wait_ge(S.gz, 3)
-    seen = [0, 0]
-
-    def got(s, k):
+            for i in range(L - 1):
+                if (k, s) == at_out(i):
+                    A.wait_ge(S.pzd, i + 1)
+                    A.activation(T.cs[:, i, :], out[i % 2][:, 0:64], COPY).then_inc(S.ccd, 1)
+            for i in range(L):
+                if (k, s) == at_t1(i):
+                    A.wait_ge(S.t1d, i + 1)
+                    A.activation(T.c1[:, i, :], pack[1][i % 2][:, 0:64], COPY).then_inc(S.ct1, 1)
+    A.wait_ge(S.mx, N)
+    A.activation(T.cs[0:64, L, :], T.cm[0:64, L, :], COPY, scale=1.0 / 8192).then_inc(S.cy7, 1)
+    P.wait_ge(S.gw, ngw)
+    P.wait_ge(S.nod, 1)
+    todo = [((v - 1 - t) // 2, s, t, v) for v in range(NU) for s in range(2) for t in range(2)]
+    todo += [at_max(i)[:1] + (0, 2, i) for i in range(L - 1)]
+    todo += [divmod(2 * at[1][0] + at[1][1] - 1, 2) + (3, 0) for at in LATER[1:]]
+    seen, done = [0, 0], {}
+    for k, s, t, v in sorted(todo):
+        if t == 3:
+            shift(2)
+            continue
+        if t == 2:
+            if v == 0:
+                P.wait_ge(S.ddn, 2)
+            if v >= 2:
+                P.wait_ge(S.ccd, v - 1)
+            P.wait_ge(S.mx, v + 1)
+            P.matmul(out[v % 2][:, 0:64], T.dm[:], T.cm[:, v, :], True, True).then_inc(S.pzd, 1)
+            continue
+        i = v // 4
+        j = done[i, t] = done.get((i, t), 0) + 1
+        if j == 1 and i >= 2:
+            P.wait_ge((S.mx, S.ct1)[t], i - 1)
         if k + 1 > seen[s]:
             P.wait_ge(S["ga%d" % s], k + 1)
             seen[s] = k + 1
+        b = 128 * v + 64 * (1 - t)
+        sh = 4 * s + v % 4
+        m = P.matmul(pack[t][i % 2][:, 0:64], T.ee[:, s, 8 - sh:136 - sh], T.no[:] if k < 0 else T.gg[:, s, b:b + 64], j == 1, j == 8)
+        if j == 8:
+            m.then_inc((S.t0d, S.t1d)[t], 1)
+    def ready(q, r):
+        if r < L - 1:
+            q.wait_ge(S.ccd, r + 1)
+        else:
+            q.wait_ge(S.cc7, r - L + 3)
+        if r == L:
+            q.wait_ge(S.cy7, 1)
 
-    def pk(i):
-        out = (T.qa, T.qb)[i % 2][:, 0:128]
-        if i >= 2:
-            P.wait_ge(S.mx, i - 1)
-        for j in range(4):
-            for s in range(2):
-                v = 4 * i + j
-                got(s, (v - 1) // 2)
-                sh = 4 * s + j
-                m = P.matmul(out, T.ee[:, s, 8 - sh:136 - sh], T.gg[:, s, 128 * v:128 * v + 128], j + s == 0, j + s == 4)
-        m.then_inc(S.td, 1)
-
-    def half(i, t, vs_, first, last):
-        out = (t0, t1)[t](i)
-        todo = [(v, s, e) for v in vs_ for s in range(2) for e in range(2)]
-        for j, (v, s, e) in enumerate(todo):
-            got(s, (v - 2) // 2 if v % 2 == 0 else (v - 1) // 2 - t)
-            sh = 4 * s + (v - blk(i)[1][0]) * 2 + e
-            b = 128 * v + 64 * (1 - t) + 32 * e
-            m = P.matmul(out, T.ee[:, s, 8 - sh:136 - sh], T.gg[:, s, b:b + 32], first and j == 0, last and j == len(todo) - 1)
-        if last:
-            m.then_inc(S.t1d if t else S.t0d, 1)
-
-    def decode(i):
-        w = blk(i)[2]
-        if i == 0:
-            P.wait_ge(S.ddn, 1)
-        P.wait_ge(S.mx, i + 1)
-        if i >= 2:
-            P.wait_ge(S.ccd, i - 1)
-        P.matmul((T.pz, T.ab)[i % 2][:, 0:w], T.dm[:], T.cm[:, i % 2, 0:w], True, True).then_inc(S.pzd, 1)
-
-    for i in range(L - 1):
-        pk(i)
-        decode(i)
-    pk(6)
-    half(7, 1, [28, 29], True, True)
-    half(7, 0, [28], True, False)
-    half(7, 0, [29], False, True)
-    half(8, 1, [30, 31], True, True)
-    decode(6)
-    half(8, 0, [30], True, False)
-    decode(7)
-    half(8, 0, [31], False, True)
-    decode(8)
-
-    def send(r, dst, src_, sem):
-        rid, pid = did(r)
-        g.remote_dma(out_ap=dst, in_ap=src_, remote_sem=sem, local_sem=S.snt, pid=pid, routing_id=rid, dma_engine_mask=emask(r))
-        return 8
-
-    for r in range(L):
-        g.wait_ge(S.ccd, r + 1)
+    for r in range(N):
+        ready(g, r)
         if r != me:
-            nsnt += send(r, T.dy[me], T.cs[:, r, :], S.rin)
-    g.wait_ge(S.cc1, 1)
-    if me != L:
-        nsnt += send(L, T.dy1[me], T.cs1[:], S.rin1)
-    g.wait_ge(S.cc2, 1)
-    if me != L:
-        nsnt += send(L, T.dy2[me], T.cs2[:], S.rin2)
-    Q.wait_ge(S.dgh, 1)
-    Q.dma_start(T.xd[:, 0:64, :], T.xh[:]).then_inc(S.xds, 16)
+            rid, pid = did(r)
+            g.remote_dma(out_ap=T.dy[me], in_ap=T.cs[:, r, :], remote_sem=S.rin, local_sem=S.snt, pid=pid, routing_id=rid, dma_engine_mask=emask(r))
+            nsnt += 8
+    def dfill(c0, n):
+        for w, m in pieces(4 * H - DA - DB + c0, 4 * H - DA - DB + c0 + n, SEED):
+            Q.dma_start(w, T.win1[:, 0:m]).then_inc(S.pl, 16)
+
+    Q.wait_ge(S.half, 1)
+    Q.wait_ge(S.seed, 1)
+    dfill(0, DA)
     Q.wait_ge(S.dgl, 1)
-    Q.dma_start(T.xd[:, 64:128, :], T.xl[:]).then_inc(S.xds, 16)
+    Q.dma_start(T.xd[:], T.xp[:]).then_inc(S.xds, 16)
 
     def landed(rs):
-        for r in rs:
+        for r in sorted(rs, key=lambda r: r != me):
             if r != me:
                 Q.wait_ge(S["xk%d" % r], 1)
-                land(r)
+            land(r)
 
+    if me < 2:
+        Q.wait_ge(S["xk%d" % (1 - me)], 1)
     landed(range(2))
-    Q.wait_ge(S.vz, 1)
-    Q.wait_ge(S.ili, 1)
-    Q.dma_start(T.vv[0:128:8, :], T.li[:]).then_inc(S.pl, 16)
+    Q.dma_start(T.vv[1:128:2, 0:512], T.win1[0:64, 0:512]).then_inc(S.pl, 16)
     Q.wait_ge(S.rbd, 1)
-    Q.dma_start(T.vv[1:128:8, :], T.rb[:]).then_inc(S.pl, 16)
+    Q.dma_start(T.vv[4:128:8, 0:512], T.rb[0:32, :]).then_inc(S.pl, 16)
+    Q.wait_ge(S.ili, 1)
+    Q.dma_start(T.vv[0:128:8, 0:512], T.li[0:32, :]).then_inc(S.pl, 16)
+    dfill(DA, DB)
     for r in range(N):
-        if r == 2:
-            landed(range(2, N))
+        for part, (r0, r1) in enumerate(PARTS):
+            if part and r == r0:
+                landed(range(r0, r1))
+                sem = S["pl%d" % part]
+                Q.wait_ge(S.xds, 16)
+                Q.dma_start(T.vv[0:128:8, 256 * r0:256 * r1], T.li[0:16 * (r1 - r0), :]).then_inc(sem, 16)
+                for c in range(r0 // 2, r1 // 2):
+                    Q.dma_start(T.vv[4:128:8, 512 * c:512 * c + 512], T.rb[32 * c:32 * c + 32, :]).then_inc(sem, 16)
+                for c in range(r0, r1, 4):
+                    Q.dma_start(T.vv[1:128:2, 256 * c:256 * min(c + 4, r1)], T.xd[0:2 * (min(c + 4, r1) - c)]).then_inc(sem, 16)
         if r != me:
             Q.wait_ge(S["xi%d" % r], 1)
-        for e, own in enumerate((T.xh, T.xl)):
-            part = own[16 * me:16 * me + 16, :] if r == me else T.d2[r, 64 * e:64 * e + 64, :]
-            Q.dma_start(T.vv[2 + e:128:8, 256 * r:256 * r + 256], part).then_inc(S["v%d" % r], 16)
-    outs = (T.y, T.z)
-    if me != L:
-        Q.wait_ge(S.ccd, me + 1)
-        Q.dma_start(T.dy[me], T.cs[:, me, :]).then_inc(S.lo, 16)
-        for k, q, sem in ((0, Q, S.st), (1, A, S.st2)):
-            q.wait_ge(S.lo, 16)
-            q.wait_ge(S.rin, 8 * len(dests))
-            for h in range(2):
-                q.dma_start(outs[k][64 * h:64 * h + 64, :], T.dy[:, 64 * k + 32 * h:64 * k + 32 * h + 32, :]).then_inc(sem, 16)
-            q.wait_ge(sem, 32)
-    else:
-        Q.wait_ge(S.cc1, 1)
-        Q.dma_start(T.dy1[me], T.cs1[:]).then_inc(S.lo1, 16)
-        Q.wait_ge(S.cc2, 1)
-        Q.dma_start(T.dy2[me], T.cs2[:]).then_inc(S.lo2, 16)
-        for k, q, sem in ((0, Q, S.st), (1, A, S.st2)):
-            done = 0
-            for b, d, lo, rin in ((0, T.dy1, S.lo1, S.rin1), (128, T.dy2, S.lo2, S.rin2)):
-                q.wait_ge(lo, 16)
-                q.wait_ge(rin, 8 * len(dests))
-                for h in range(2):
-                    q.dma_start(outs[k][64 * h:64 * h + 64, b:b + 128], d[:, 64 * k + 32 * h:64 * k + 32 * h + 32, :]).then_inc(sem, 16)
-                    done += 16
-            q.wait_ge(sem, done)
+        Q.dma_start(T.vv[2:128:4, 256 * r:256 * r + 256], T.xp[16 * me:16 * me + 16] if r == me else T.d2[r]).then_inc(S["v%d" % r], 16)
+    ready(Q, me)
+    Q.dma_start(T.dy[me], T.cs[:, me, :]).then_inc(S.lo, 16)
+    for o, k, q, sem in ((T.y, 0, Q, S.st), (T.z, 1, A, S.st2)):
+        q.wait_ge(S.lo, 16)
+        q.wait_ge(S.rin, 8 * len(dests))
+        for h in range(2):
+            q.dma_start(o[64 * h:64 * h + 64, :], T.dy[:, 64 * k + 32 * h:64 * k + 32 * h + 32, :]).then_inc(sem, 16)
+        q.wait_ge(sem, 32)
     g.wait_ge(S.snt, nsnt)

from concourse.bass import DstId, RemoteDMATransfer
from concourse.mybir import AluOpType, ActivationFunctionType

N, T_, R, H = 8, 256, 64, 4096
NU = N * T_ // R
NK = NU // 2
COPY, RELU = ActivationFunctionType.Copy, ActivationFunctionType.Relu
BF = "bfloat16"
SEED, VA, VB, VC = 1024, 512, 5376, 1024
DA, DB = 2048, 0
AF = 4 * H - SEED - VA - VB - VC - DA - DB
LATER = (((0, 1), (1, 0), (1, 1), (1, 1), (2, 0), (2, 1)), ((3, 1), (4, 0), (4, 1), (5, 1), (6, 0), (6, 1)))
PARTS = ((0, 2), (2, 4), (4, 8))
FIN = 4

SCRATCH = {
    "xs": ("dram", [8, 128, 32], "int32"),
    "d1": ("dram", [8, 128, 32], "int32"),
    "xd": ("dram", [8, 128, 64], BF),
    "d2": ("dram", [8, 128, 64], BF),
    "dy": ("dram", [8, 128, 64], "float32"),
    "xq": ("sbuf", [128, 256], "int32"),
    "xp": ("sbuf", [128, 2, 256], BF),
    "lnd": ("sbuf", [128, 256], "int32"),
    "tt": ("sbuf", [128, 8, 2, 16], "int32"),
    "xa": ("sbuf", [128, 2, 144], "float32"), "xb": ("sbuf", [128, 2, 128], "float32"),
    "one": ("sbuf", [128, 256], BF),
    "sel": ("sbuf", [128, 128], "float32"),
    "hs": ("sbuf", [128, 4], "int32"),
    "hsf": ("sbuf", [128, 4], "float32"),
    "m0": ("sbuf", [128, 128], "float32"),
    "m1": ("sbuf", [128, 8, 16], "float32"),
    "mw": ("sbuf", [128, 128], "float32"),
    "dm": ("sbuf", [128, 128], "float32"),
    "pi": ("sbuf", [128, 32], BF), "pr": ("sbuf", [128, 32], BF),
    "li": ("sbuf", [128, 256], BF), "rb": ("sbuf", [128, 256], BF),
    "ee": ("sbuf", [128, 2, 144], BF),
    "no": ("sbuf", [128, 64], BF),
    "vv": ("sbuf", [128, 2048], BF),
    "ki": ("sbuf", [128, 2, 16, 8], "int32"), "kj": ("sbuf", [128, 2, 16, 8], "int32"),
    "ll": ("sbuf", [128, 2, 17, 16], "uint16"),
    "win0": ("sbuf", [128, 2 * H], BF), "win1": ("sbuf", [128, 2 * H], BF),
    "gg": ("sbuf", [128, 2, 4096], BF),
    "c1": ("sbuf", [128, 8, 64], "float32"), "cm": ("sbuf", [128, 8, 64], "float32"),
    "za": ("psum", [128, 512], "float32"), "zb": ("psum", [128, 512], "float32"),
    "cs": ("sbuf", [128, 8, 64], "float32"),
    "ab": ("psum", [128, 512], "float32"), "ps": ("psum", [128, 512], "float32"),
    "qa": ("psum", [128, 512], "float32"), "qb": ("psum", [128, 512], "float32"),
    "ua": ("psum", [128, 512], "float32"), "ub": ("psum", [128, 512], "float32"),
}
SEMAPHORES = (["x1", "x2", "hcl", "lk0", "lk1", "lk2", "pl1", "snt", "rin",
               "ipi", "ili", "half", "gw", "gl", "gm", "vi", "vf", "seed", "ones", "rdy", "pab", "msk", "nod",
               "ddn", "idn", "sfl", "dgh", "dgl", "xds", "rbd", "pl", "pl2", "xf", "kp", "sc0", "sc1", "ga0", "ga1",
               "t0d", "t1d", "ct1", "c17", "mx", "cy7", "pzd", "ccd", "cc7", "lo", "st", "st2"]
              + ["v%d" % r for r in range(8)] + ["xi%d" % r for r in range(8)] + ["xk%d" % r for r in range(8)])


def rank_program(g, core, T, topo):
    me = T.rank_of(core)
    if me is None:
        return
    S = T.sem
    V, A, P, Q = g.vector, g.scalar, g.tensor, g.sync
    A_ = AluOpType
    others = [r for r in range(N) if r != me]
    offchip = [r for r in others if topo.chip(T.cores[r]) != topo.chip(core)]
    onchip = [r for r in others if topo.chip(T.cores[r]) == topo.chip(core)]
    dests = offchip + onchip
    L = N - 1

    def did(r):
        rid, pid, _ = topo.addr(T.cores[r])
        return rid, pid

    def eng(r, k):
        e = topo.engines(core, T.cores[r])[:8]
        return 1 << e[k % len(e)]

    def emask(r):
        m = 0
        for e in topo.engines(core, T.cores[r])[:8]:
            m |= 1 << e
        return m

    def pieces(c0, c1, most):
        while c0 < c1:
            c = min(c1, c0 + most, (c0 // (2 * H) + 1) * 2 * H)
            yield T["win%d" % (1 - c0 // (2 * H))][:, c0 % (2 * H):(c - 1) % (2 * H) + 1], c - c0
            c0 = c

    def rows(q, h, c):
        q.dma_start(T.xq[2 * h + c:128:4, :], T.x[64 * h + c:64 * h + 64:2, :]).then_inc(S.x2, 16)

    for h, q in ((0, Q), (1, A)):
        q.dma_start(T.xs[:, 64 * h:64 * h + 64, :], T.x[64 * h:64 * h + 64, :]).then_inc(S.x1, 16)
    for c in range(2):
        rows(Q, 0, c)
        rows(A, 1, c)
    for h in range(2):
        Q.dma_start(T.hs[h:8:2, :], T.hc[64 * h + 8 * me:64 * h + 8 * me + 8, :]).then_inc(S.hcl, 16)

    def land(r):
        for h in range(2):
            src = T.x[64 * h + 8 * me:64 * h + 8 * me + 8, :] if r == me else T.d1[r, 64 * h:64 * h + 64, :]
            Q.dma_start(T.lnd[:, 32 * r + 16 * h:32 * r + 16 * h + 16], src).then_inc(S["lk%d" % [r0 <= r < r1 for r0, r1 in PARTS].index(True)], 16)

    g.iota(T.pi[:], [[0, 16], [256, 2]], 0, 16, allow_small_or_imprecise_dtypes=True).then_inc(S.ipi, 1)
    g.wait_ge(S.ones, 1)
    g.affine_select(T.m1[:, :, 1:16], T.one[:, 0:120], [[16, 8], [1, 15]], A_.is_equal, 0.0, 0, -1).then_inc(S.msk, 1)
    g.affine_select(T.m1[:, :, 0], T.one[:, 0:8], [[0, 8]], A_.is_gt, 0.0, 0, 0).then_inc(S.msk, 1)

    def all_to_all(src, dst, sem, k0):
        tr = []
        for k, r in enumerate(dests):
            rid, pid = did(r)
            tr.append(RemoteDMATransfer(src=src[r], dst=dst[me], dst_ids=[DstId(rid=rid, pnc=pid)],
                                        dma_engine_mask=eng(r, k + k0), remote_sem=sem))
        g.remote_dma_fused(tr, local_sem=S.snt)

    g.wait_ge(S.x1, 32)
    all_to_all(T.xs, T.d1, S["xk%d" % me], 0)

    def parts_out():
        g.wait_ge(S.xds, 16)
        all_to_all(T.xd, T.d2, S["xi%d" % me], 5)

    g.affine_select(T.sel[0:8, :], T.one[0:8, 0:128], [[1, 8], [0, 16]], A_.is_equal, 0.0, 0, -1).then_inc(S.rdy, 1)
    if me < 2:
        parts_out()
    g.affine_select(T.mw[:], T.one[:, 0:128], [[16, 8], [1000, 16]], A_.is_equal, 0.0, 15, -1).then_inc(S.msk, 1)
    g.affine_select(T.xa[:, :, 15], T.one[:, 0:2], [[0, 2]], A_.is_gt, 0.0, 0, 0).then_inc(S.msk, 1)
    nsnt = 2 * len(dests)
    lanes = [[-8, 2], [-16, 2], [-32, 4]]
    g.iota(T.ee[:], [[0, 288]], 0, 0, allow_small_or_imprecise_dtypes=True).then_inc(S.gw, 1)
    g.wait_ge(S.ili, 1)
    g.affine_select(T.no[:], T.li[:, 0:64], [[0, 64]], A_.is_gt, -0.5, 0, 0).then_inc(S.nod, 1)
    if me >= 2:
        g.wait_ge(S.lk0, 64)
        parts_out()
    yp, ps = (T.ee[:, :, 8:72:8], T.ee[:, :, 72:136:8]), (T.ee[:, :, 72:136:8],)
    ngw = 1
    for rnd in ([(yp, 0, 8192)], [(yp, 4, 8192)], [(ps, 2, 1)], [(ps, 6, 1)]):
        g.wait_ge(S.gw, ngw)
        for to, lane, w in rnd:
            for half in to:
                g.affine_select(half, half, lanes, A_.not_equal, float(w), -lane, 1).then_inc(S.gw, 1)
                ngw += 1
    g.affine_select(T.m0[:], T.one[:, 0:128], [[1, 128]], A_.is_equal, 0.0, 0, -1).then_inc(S.idn, 1)
    g.wait_ge(S.idn, 1)
    g.affine_select(T.dm[:, 0:64], T.m0[:, 0:64], [[1, 64]], A_.not_equal, 1.0 / 8192, 0, -1).then_inc(S.ddn, 1)
    g.affine_select(T.dm[:, 64:128], T.m0[:, 64:128], [[1, 64]], A_.not_equal, -1.0, 0, -1).then_inc(S.ddn, 1)

    nvi, nvf = [0], [0]

    def vi(ins):
        ins.then_inc(S.vi, 1)
        nvi[0] += 1

    def vs():
        V.wait_ge(S.vi, nvi[0])

    def fill(c0, n):
        c0 += SEED + AF
        for w, _ in pieces(c0, c0 + n, 2 * H):
            V.memset(w, -0.5).then_inc(S.vf, 1)
            nvf[0] += 1

    V.memset(T.one[:], 1.0).then_inc(S.ones, 1)
    V.memset(T.win1[:, 0:SEED // 2], -0.5).then_inc(S.half, 1)
    V.memset(T.win1[:, SEED // 2:SEED], -0.5).then_inc(S.seed, 1)
    V.wait_ge(S.ipi, 1)
    vi(V.transpose(T.pr[:], T.pi[:]))
    V.wait_ge(S.ones, 1)
    V.tensor_tensor_scan(T.li[:], T.one[:], T.one[:], -2, A_.mult, A_.add).then_inc(S.ili, 1)
    V.wait_ge(S.half, 1)
    vs()
    V.tensor_scalar(T.rb[:], T.win1[:, 0:256], 0, T.pr[:, 0:1], A_.mult, A_.add).then_inc(S.rbd, 1)
    fill(0, VA)
    V.wait_ge(S.x2, 64)
    V.tensor_copy(T.xp[:, 0, :], T.xq[:]).then_inc(S.dgh, 1)
    V.wait_ge(S.hcl, 32)
    V.tensor_copy(T.hsf[0:8, :], T.hs[0:8, :]).then_inc(S.rdy, 1)
    V.wait_ge(S.dgh, 1)
    V.tensor_tensor(T.xp[:, 1, :], T.xq[:], T.xp[:, 0, :], A_.subtract).then_inc(S.dgl, 1)
    fill(VA, VB)
    P.wait_ge(S.rdy, 2)
    P.matmul(T.ab[:, 0:4], T.sel[0:8, :], T.hsf[0:8, :], True, True).then_inc(S.pab, 1)
    A.wait_ge(S.half, 1)
    A.activation(T.win1[:, SEED:SEED + SEED // 2], T.win1[:, 0:SEED // 2], COPY).then_inc(S.sfl, 1)
    A.wait_ge(S.seed, 1)
    nsf = 1
    for w, n in pieces(SEED + SEED // 2, SEED + AF, SEED):
        A.activation(w, T.win1[:, 0:n], COPY).then_inc(S.sfl, 1)
        nsf += 1

    P.wait_ge(S.msk, 4)

    def shift(part):
        c0, c1 = 16 * PARTS[part][0], 16 * PARTS[part][1]
        P.wait_ge(S.xf, 2 * part + 2)
        P.matmul(T.ps[:, 2 * c0:2 * c1], T.m1[:], T.xa[:, :, 16 + c0:16 + c1], True, False)
        P.matmul(T.ps[:, 2 * c0:2 * c1], T.mw[:], T.xa[:, :, 15 + c0:15 + c1], False, True).then_inc(S.kp, 1)

    shift(0)
    shift(1)

    def flip(part):
        r0, r1 = PARTS[part]
        V.wait_ge(S["lk%d" % part], 32 * (r1 - r0))
        vi(V.transpose(T.tt[:, r0:r1, :, :], T.lnd[:, 32 * r0:32 * r1]))

    def times_a(part):
        r0, r1 = PARTS[part]
        vs()
        for s in range(2):
            V.tensor_scalar(T.xa[:, s, 16 + 16 * r0:16 + 16 * r1], T.tt[:, r0:r1, s, :], T.ab[:, 2 * s:2 * s + 1], None, A_.mult).then_inc(S.xf, 1)

    def times_b(part):
        r0, r1 = PARTS[part]
        for s in range(2):
            vi(V.tensor_scalar(T.xb[:, s, 16 * r0:16 * r1], T.tt[:, r0:r1, s, :], T.ab[:, 2 * s + 1:2 * s + 2], None, A_.mult))

    def whole(part):
        r0, r1 = PARTS[part]
        vs()
        V.wait_ge(S.kp, part + 1)
        vi(V.tensor_tensor(T.ki[:, :, 2 * r0:2 * r1, :], T.ps[:, 32 * r0:32 * r1], T.xb[:, :, 16 * r0:16 * r1], A_.add))

    def key(part):
        r0, r1 = PARTS[part]
        vs()
        vi(V.tensor_scalar(T.kj[:, :, 2 * r0:2 * r1, :], T.ki[:, :, 2 * r0:2 * r1, :], 9, H - 1, A_.logical_shift_right, A_.bitwise_and))

    def lists(part):
        c0, c1 = 2 * PARTS[part][0], 2 * PARTS[part][1]
        even, odd = T.kj[:, :, c0:c1, 0:4], T.kj[:, :, c0:c1, 4:8]
        vs()
        V.tensor_copy(T.ll[:, :, c0:c1, 8:12], even).then_inc(S.gl, 1)
        V.tensor_scalar(T.ll[:, :, c0:c1, 12:16], odd, H, None, A_.add).then_inc(S.gl, 1)
        V.tensor_copy(T.ll[:, :, c0 + 1:c1 + 1, 0:4], odd).then_inc(S.gm, 1)
        V.tensor_scalar(T.ll[:, :, c0:c1, 4:8], even, H, None, A_.add).then_inc(S.gm, 1)

    flip(0)
    V.wait_ge(S.pab, 1)
    times_a(0)
    times_b(0)
    fill(VA + VB, VC)
    whole(0)
    key(0)
    lists(0)
    pack, out = ((T.qa, T.qb), (T.ua, T.ub)), (T.za, T.zb)

    def at_t1(i):
        return (max(2 * i + 1, 2), 1)

    def at_max(i):
        return (min(max(2 * i + 2, 3), NK - 1), 1)

    def at_out(i):
        return (max(2 * i + 3, 4), 0)

    def vmax(i):
        if i == L:
            V.wait_ge(S.t1d, N)
            V.tensor_copy(T.c1[:, L, :], pack[1][L % 2][:, 0:64]).then_inc(S.c17, 1)
            V.wait_ge(S.c17, 1)
        else:
            V.wait_ge(S.ct1, i + 1)
        V.wait_ge(S.t0d, i + 1)
        V.tensor_tensor(T.cm[:, i, :], T.c1[:, i, :], pack[0][i % 2][:, 0:64], A_.max).then_inc(S.mx, 1)
        if i >= L - 1:
            V.wait_ge(S.mx, i + 1)
            V.tensor_tensor(T.cs[64:128, i, :], T.cm[64:128, i, :], T.cm[0:64, i, :], A_.subtract).then_inc(S.cc7, 1)
        if i == L - 1:
            V.tensor_scalar(T.cs[0:64, i, :], T.cm[0:64, i, :], 1.0 / 8192, None, A_.mult).then_inc(S.cc7, 1)

    V.wait_ge(S.vf, nvf[0])
    V.wait_ge(S.pl, 16 * (3 + (DA + DB) // SEED))
    V.wait_ge(S.gl, 2)
    between = [(at, step, part) for part in range(1, len(PARTS)) for at, step in zip(LATER[part - 1], (flip, times_a, times_b, whole, key, lists))]
    between += [(at_max(i), vmax, i) for i in range(N)]
    for k in range(NK):
        n = 128 if k < NK - 1 else 64
        for s in range(2):
            if s == 0 and (k == 0 or (k % 2 == 1 and k < NK - 1)):
                V.wait_ge(S["v%d" % ((k + 1) // 2)], 16)
            for part, (r0, r1) in enumerate(PARTS):
                if part and (k, s) == (2 * r0 - 1, 0):
                    V.wait_ge(S["pl%d" % part], 16 * (1 + (r1 - r0) // 2 + (r1 - r0 + 3) // 4))
                if part and (k, s) == (2 * r0, 0):
                    V.wait_ge(S.gl, 2 * part + 2)
            if (k, s) == (0, 1):
                V.wait_ge(S.sfl, nsf)
            if k:
                V.wait_ge(S["ga%d" % s], k)
            V.tensor_copy(T["win%d" % s][:].indirect(T.ll[:, s, k, 8:8 + n // 16]),
                          T.vv[:, 128 * k + 1:128 * k + 1 + n]).then_inc(S["sc%d" % s], 1)
            for at, step, arg in between:
                if at == (k, s):
                    step(arg)
    for k in range(NK):
        n = 256 if k < NK - 1 else 64
        for s in range(2):
            A.wait_ge(S["sc%d" % s], k + 1)
            for part, (r0, r1) in enumerate(PARTS):
                if (k, s) == (max(2 * r0 - 1, 0), 0):
                    A.wait_ge(S.gl, 2 * part + 2)
                    A.wait_ge(S.gm, 2 * part + 2)
            A.activation(T.gg[:, s, 256 * k + 192:256 * k + 192 + n],
                         T["win%d" % s][:].indirect(T.ll[:, s, k + 1, 0:n // 16]), COPY).then_inc(S["ga%d" % s], 1)
            for i in range(L - 1):
                if (k, s) == at_out(i):
                    A.wait_ge(S.pzd, i + 1)
                    A.activation(T.cs[:, i, :], out[i % 2][:, 0:64], COPY).then_inc(S.ccd, 1)
            for i in range(L):
                if (k, s) == at_t1(i):
                    A.wait_ge(S.t1d, i + 1)
                    A.activation(T.c1[:, i, :], pack[1][i % 2][:, 0:64], COPY).then_inc(S.ct1, 1)
    A.wait_ge(S.mx, N)
    A.activation(T.cs[0:64, L, :], T.cm[0:64, L, :], COPY, scale=1.0 / 8192).then_inc(S.cy7, 1)
    P.wait_ge(S.gw, ngw)
    P.wait_ge(S.nod, 1)
    todo = [((v - 1 - t) // 2, s, t, v) for v in range(NU) for s in range(2) for t in range(2)]
    todo += [at_max(i)[:1] + (0, 2, i) for i in range(L - 1)]
    todo += [divmod(2 * at[1][0] + at[1][1] - 1, 2) + (3, 0) for at in LATER[1:]]
    seen, done = [0, 0], {}
    for k, s, t, v in sorted(todo):
        if t == 3:
            shift(2)
            continue
        if t == 2:
            if v == 0:
                P.wait_ge(S.ddn, 2)
            if v >= 2:
                P.wait_ge(S.ccd, v - 1)
            P.wait_ge(S.mx, v + 1)
            P.matmul(out[v % 2][:, 0:64], T.dm[:], T.cm[:, v, :], True, True).then_inc(S.pzd, 1)
            continue
        i = v // 4
        j = done[i, t] = done.get((i, t), 0) + 1
        if j == 1 and i >= 2:
            P.wait_ge((S.mx, S.ct1)[t], i - 1)
        if k + 1 > seen[s]:
            P.wait_ge(S["ga%d" % s], k + 1)
            seen[s] = k + 1
        b = 128 * v + 64 * (1 - t)
        sh = 4 * s + v % 4
        m = P.matmul(pack[t][i % 2][:, 0:64], T.ee[:, s, 8 - sh:136 - sh], T.no[:] if k < 0 else T.gg[:, s, b:b + 64], j == 1, j == 8)
        if j == 8:
            m.then_inc((S.t0d, S.t1d)[t], 1)
    def ready(q, r):
        if r < L - 1:
            q.wait_ge(S.ccd, r + 1)
        else:
            q.wait_ge(S.cc7, r - L + 3)
        if r == L:
            q.wait_ge(S.cy7, 1)

    for r in range(N):
        ready(g, r)
        if r != me:
            rid, pid = did(r)
            g.remote_dma(out_ap=T.dy[me], in_ap=T.cs[:, r, :], remote_sem=S.rin, local_sem=S.snt, pid=pid, routing_id=rid, dma_engine_mask=emask(r))
            nsnt += 8
    def dfill(c0, n):
        for w, m in pieces(4 * H - DA - DB + c0, 4 * H - DA - DB + c0 + n, SEED):
            Q.dma_start(w, T.win1[:, 0:m]).then_inc(S.pl, 16)

    Q.wait_ge(S.half, 1)
    Q.wait_ge(S.seed, 1)
    dfill(0, DA)
    Q.wait_ge(S.dgl, 1)
    Q.dma_start(T.xd[:], T.xp[:]).then_inc(S.xds, 16)

    def landed(rs):
        for r in sorted(rs, key=lambda r: r != me):
            if r != me:
                Q.wait_ge(S["xk%d" % r], 1)
            land(r)

    if me < 2:
        Q.wait_ge(S["xk%d" % (1 - me)], 1)
    landed(range(2))
    Q.dma_start(T.vv[1:128:2, 0:512], T.win1[0:64, 0:512]).then_inc(S.pl, 16)
    Q.wait_ge(S.rbd, 1)
    Q.dma_start(T.vv[4:128:8, 0:512], T.rb[0:32, :]).then_inc(S.pl, 16)
    Q.wait_ge(S.ili, 1)
    Q.dma_start(T.vv[0:128:8, 0:512], T.li[0:32, :]).then_inc(S.pl, 16)
    dfill(DA, DB)
    for r in range(N):
        for part, (r0, r1) in enumerate(PARTS):
            if part and r == r0:
                landed(range(r0, r1))
                sem = S["pl%d" % part]
                Q.wait_ge(S.xds, 16)
                Q.dma_start(T.vv[0:128:8, 256 * r0:256 * r1], T.li[0:16 * (r1 - r0), :]).then_inc(sem, 16)
                for c in range(r0 // 2, r1 // 2):
                    Q.dma_start(T.vv[4:128:8, 512 * c:512 * c + 512], T.rb[32 * c:32 * c + 32, :]).then_inc(sem, 16)
                for c in range(r0, r1, 4):
                    Q.dma_start(T.vv[1:128:2, 256 * c:256 * min(c + 4, r1)], T.xd[0:2 * (min(c + 4, r1) - c)]).then_inc(sem, 16)
        if r != me:
            Q.wait_ge(S["xi%d" % r], 1)
        Q.dma_start(T.vv[2:128:4, 256 * r:256 * r + 256], T.xp[16 * me:16 * me + 16] if r == me else T.d2[r]).then_inc(S["v%d" % r], 16)
    ready(Q, me)
    Q.dma_start(T.dy[me], T.cs[:, me, :]).then_inc(S.lo, 16)
    for o, k, q, sem in ((T.y, 0, Q, S.st), (T.z, 1, A, S.st2)):
        q.wait_ge(S.lo, 16)
        q.wait_ge(S.rin, 8 * len(dests))
        for h in range(2):
            q.dma_start(o[64 * h:64 * h + 64, :], T.dy[:, 64 * k + 32 * h:64 * k + 32 * h + 32, :]).then_inc(sem, 16)
        q.wait_ge(sem, 32)
    g.wait_ge(S.snt, nsnt)
